import numpy as np
import ml_dtypes


def mxq(x, axis, fmt="e4m3"):
    dtype, down = {"e4m3": (ml_dtypes.float8_e4m3fn, 7), "e5m2": (ml_dtypes.float8_e5m2, 14)}[fmt]
    v = np.moveaxis(np.asarray(x, np.float32).astype(ml_dtypes.bfloat16).astype(np.float64), axis, -1)
    blocks = v.reshape(v.shape[:-1] + (-1, 32))
    amax = np.abs(blocks).max(-1, keepdims=True)
    byte = np.maximum(np.where(amax > 0, np.frexp(amax)[1] - 1 + 127, 0) - down, 1)
    scale = np.exp2(byte - 127.0)
    codes = (blocks / scale).astype(np.float32).astype(dtype).astype(np.float64)
    return np.moveaxis((codes * scale).reshape(v.shape), -1, axis)


WIDE = False


def mx_kscale(k):
    if not WIDE:
        return np.ones(k)
    levels = np.array([18, -18])
    if k % 512:
        return np.exp2(np.random.permutation(np.resize(levels, k // 32))).repeat(32)
    a = np.empty((k // 512, 16))
    for p in range(k // 512):
        a[p, :8] = np.random.permutation(np.resize(levels, 8))
        for g in range(8):
            far = levels[np.abs(levels - a[p, g]) >= 10]
            a[p, g + 8] = far[np.random.randint(len(far))]
    return np.exp2(a.ravel()).repeat(32)


def f64(x):
    return np.asarray(x).astype(np.float64)


def striped(idx):
    return np.tile(np.asarray(idx).reshape(-1, 16).T, (8, 1)).astype(np.uint16)


def unstriped(offs):
    return offs[:16].T.reshape(-1).astype(np.int64)

def planes(y):
    n, m = y.shape
    v = y.astype(np.float32).astype(ml_dtypes.bfloat16).astype(np.float64).reshape(n // 32, 32, m)
    top = np.abs(v).max(1)
    byte = np.clip(np.where(top > 0, np.frexp(top)[1] - 1 + 127 - 7, 1), 1, 254)
    codes = (v * np.exp2(127.0 - byte)[:, None, :]).reshape(n, m).astype(np.float32).astype(ml_dtypes.float8_e4m3fn).view(np.uint8)
    words = codes.reshape(n // 512, 128, 4, m).transpose(0, 1, 3, 2)
    return np.ascontiguousarray(words), np.ascontiguousarray(byte.astype(np.uint8).reshape(n // 512, 16, m))


B, N, T, D, R = 1, 512, 2048, 512, 1024


def setup_inputs():
    n = np.random.standard_normal
    idx = np.random.permutation(T)[:B * N]
    s = mx_kscale(D)[:, None]
    u = np.ones(T)
    u[idx] = mx_kscale(B * N)
    r = np.random.uniform(0.5, 2.0, T) * u
    x = n((B, D, R))
    return {
        "xT": (x * s).astype(np.float32),
        "wT": (n((D, T)) * (1.00 / np.sqrt(D)) / s / r).astype(np.float32),
        "y": np.random.randint(0, 2, (B, R, N)).astype(np.float32),
        "wt": (np.random.uniform(0.5, 1.5, (B, R, 1)) * 1.0 / np.sqrt(R)).astype(np.float32),
        "ts": np.tile(r, (128, 1)).astype(np.float32),
        "offs": striped(idx),
    }


def reference(xT, wT, y, wt, ts, offs):
    idx = unstriped(offs)
    pick = lambda x: x[:, idx].reshape(x.shape[0], B, N).transpose(1, 0, 2)
    w = pick(f64(wT))
    a = mxq(f64(xT), 1, "e4m3").transpose(0, 2, 1) @ mxq(w, 1, "e4m3")
    ts_ = pick(f64(ts))[:, :1, :]
    a = a * ts_
    g = f64(wt) * (1.0 / (1.0 + np.exp(-a)) - f64(y))
    g = g * ts_
    gx = mxq(g, 2, "e5m2") @ mxq(w, 2, "e4m3").transpose(0, 2, 1)
    out_0 = gx
    return (out_0,) + planes(out_0[0])

@@ -1,0 +1,236 @@
+from contextlib import ExitStack
+
+import concourse.mybir as mybir
+from concourse.masks import make_identity
+
+N, T, D, R = 512, 2048, 512, 1024
+FLOPS = 2 * 2 * R * N * D
+
+F32 = mybir.dt.float32
+BF16 = mybir.dt.bfloat16
+U32 = mybir.dt.uint32
+I32 = mybir.dt.int32
+U16 = mybir.dt.uint16
+U8 = mybir.dt.uint8
+E4M3 = mybir.dt.float8_e4m3fn_x4
+E5M2 = mybir.dt.float8_e5m2_x4
+ACT = mybir.ActivationFunctionType
+ALU = mybir.AluOpType
+
+P = 128
+PACK = 4
+HALF = P * PACK
+HALVES = R // HALF
+PAIR = 2 * P
+
+
+def tile_attend_gnce_pl_x_ts_kernel(tc, xT, wT, y, wt, ts, offs, out_0, out_1, out_2):
+    nc = tc.nc
+    with ExitStack() as ctx:
+        keep = ctx.enter_context(tc.tile_pool(name="keep", bufs=1))
+        ring = ctx.enter_context(tc.tile_pool(name="ring", bufs=3))
+        psum = ctx.enter_context(tc.psum_pool(name="psum", bufs=1))
+
+        def bank(tag):
+            return psum.tile([P, HALF], F32, name=tag, tag=tag, bufs={"sc": 3, "yt": 3, "acc": 2}[tag])
+
+        offsets = keep.tile([P, N // 16], U16, name="offsets")
+        nc.sync.dma_start(offsets[:], offs)
+
+        x_view = xT[0].rearrange("(p t) r -> p t r", t=PACK)
+        w_view = wT.rearrange("(p t) c -> p t c", t=PACK)
+        y_view = y[0].rearrange("(o p j) i -> o p j i", o=HALVES, j=PACK)
+        x_raw = [keep.tile([P, PACK, HALF], F32, name=f"x_raw{o}") for o in range(HALVES)]
+        w_raw = [keep.tile([P, T], F32, name=f"w_raw{t}") for t in range(PACK)]
+        y_raw = [[keep.tile([P, 2, N], F32, name=f"y_raw{o}{a}") for a in range(2)] for o in range(HALVES)]
+
+        ts_row = keep.tile([P, T], F32, name="ts_row")
+        nc.vector.memset(ts_row[:], 0.0)
+        wt_view = wt[0].rearrange("(o p j) e -> o p (j e)", o=HALVES, j=PACK)
+        wt_sb = [keep.tile([P, PACK], F32, name=f"wt_sb{o}") for o in range(HALVES)]
+        for o in range(HALVES):
+            nc.scalar.dma_start(wt_sb[o][:], wt_view[o])
+        nc.scalar.dma_start(ts_row[0:1, :], ts[0:1, :])
+
+        for t, pieces in enumerate((4, 2, 1, 1)):
+            for c in range(pieces):
+                cols = slice(c * T // pieces, (c + 1) * T // pieces)
+                nc.sync.dma_start(w_raw[t][:, cols], w_view[:, t, cols])
+        nc.sync.dma_start(x_raw[0][:], x_view[:, :, 0:HALF])
+        for a in range(2):
+            nc.sync.dma_start(y_raw[0][a][:], y_view[0, :, 2 * a : 2 * a + 2, :])
+        nc.sync.dma_start(x_raw[1][:], x_view[:, :, HALF:R])
+        for a in range(2):
+            nc.sync.dma_start(y_raw[1][a][:], y_view[1, :, 2 * a : 2 * a + 2, :])
+
+        ident = keep.tile([P, P], F32, name="ident")
+        make_identity(nc, ident[:])
+        warm = keep.tile([P, 1], F32, name="warm")
+        nc.scalar.activation(warm[:], ident[:, 0:1], ACT.Sigmoid)
+
+        ts_listed = keep.tile([P, N], F32, name="ts_listed")
+        nc.vector.tensor_copy(ts_listed[:], ts_row[:].indirect(offsets[:]))
+        ts_bank = bank("sc")
+        for t in range(PACK):
+            nc.tensor.transpose(ts_bank[:, t * P : (t + 1) * P], ts_listed[:, t:N:PACK], ident[:])
+        ts_col = keep.tile([P, PACK], F32, name="ts_col")
+        nc.scalar.copy(ts_col[:], ts_bank[:, 0:HALF:P])
+
+        tw = [keep.tile([P, PACK, HALF], F32, name=f"tw{o}") for o in range(HALVES)]
+        for o in range(HALVES):
+            wt_bank = bank("acc")
+            for j in range(PACK):
+                nc.tensor.transpose(wt_bank[:, j * P : (j + 1) * P], wt_sb[o][:, j : j + 1].to_broadcast([P, P]), ident[:])
+            for t in range(PACK):
+                nc.scalar.activation(tw[o][:, t, :], wt_bank[:], ACT.Copy, scale=ts_col[:, t : t + 1])
+
+        def quantize(name, src, width, fmt):
+            codes = keep.tile([P, width], U32, name=name + "_codes", align_bytes=64)
+            scales = keep.tile([P, width], U8, name=name + "_scales", align_bytes=64)
+            nc.vector.quantize_mx(out=codes[:].bitcast(fmt), scales=scales[:], in_=src.rearrange("p c t -> p (c t)"))
+            return codes, scales
+
+        x_il = {}
+        xq = {}
+
+        def deal_x(o, a, copy):
+            x_il[o, a] = keep.tile([P, PAIR, PACK], BF16, name=f"x_il{o}{a}", align_bytes=64)
+            copy(
+                x_il[o, a][:].rearrange("p (j s) t -> p s t j", j=2),
+                x_raw[o][:].rearrange("p t (s j) -> p s t j", j=PACK)[:, :, :, 2 * a : 2 * a + 2],
+            )
+            xq[o, a] = quantize(f"xq{o}{a}", x_il[o, a][:], PAIR, E4M3)
+
+        w_il = keep.tile([P, N, PACK], BF16, name="w_il", align_bytes=64)
+        w_dealt = w_il[:].rearrange("p (r s) t -> p t s r", r=PACK)
+        for t in range(PACK):
+            nc.vector.tensor_copy(w_dealt[:, t], w_raw[t][:].indirect(offsets[:]))
+        wq_codes, wq_scales = quantize("wq", w_il[:], N, E4M3)
+
+        diff = {}
+
+        def score(o, a, b):
+            yt = bank("yt")
+            for tt in range(2):
+                for jj in range(2):
+                    col = (2 * tt + jj) * P
+                    nc.tensor.transpose(yt[:, col : col + P], y_raw[o][a][:, jj, 2 * b + tt : N : PACK], ident[:])
+            sc = bank("sc")
+            sig = ring.tile([P, HALF], F32, name="sig", tag="sig")
+            x_codes, x_scales = xq[o, a]
+            for tt in range(2):
+                t = 2 * b + tt
+                slots = slice(t * P, (t + 1) * P)
+                cols = slice(tt * PAIR, (tt + 1) * PAIR)
+                nc.tensor.matmul_mx(
+                    out=sc[:, cols],
+                    lhsT=wq_codes[:, slots].bitcast(E4M3), lhsT_scale=wq_scales[:, slots],
+                    rhs=x_codes[:].bitcast(E4M3), rhs_scale=x_scales[:],
+                    start=True, stop=True,
+                )
+            for tt in range(2):
+                t = 2 * b + tt
+                cols = slice(tt * PAIR, (tt + 1) * PAIR)
+                nc.scalar.activation(sig[:, cols], sc[:, cols], ACT.Sigmoid, scale=ts_col[:, t : t + 1])
+            if b == 0:
+                diff[o, a] = ring.tile([P, PACK, PAIR], F32, name="diff", tag="diff")
+            nc.vector.tensor_tensor(diff[o, a][:, 2 * b : 2 * b + 2, :].rearrange("p t c -> p (t c)"), sig[:], yt[:], ALU.subtract)
+
+        def weigh(o, a, first, count):
+            h_il = ring.tile([P, count * P, PACK], BF16, name="h_il", tag="h_il", align_bytes=64)
+            cols = slice(first * P, (first + count) * P)
+            nc.vector.tensor_tensor(
+                h_il[:].rearrange("p (c i) t -> p c t i", i=4),
+                diff[o, a][:, :, cols].rearrange("p t (c i) -> p c t i", i=4),
+                tw[o][:, :, a * PAIR : (a + 1) * PAIR][:, :, cols].rearrange("p t (c i) -> p c t i", i=4),
+                ALU.mult,
+            )
+            return h_il
+
+        out_sb = [keep.tile([P, PACK, D], F32, name=f"out_sb{o}") for o in range(HALVES)]
+        out_view = out_0[0].rearrange("(o p j) d -> o p j d", o=HALVES, j=PACK)
+
+        def back(o, j0, count, h_il):
+            h_codes, h_scales = quantize(f"hq{o}{j0}", h_il[:], count * P, E5M2)
+            for jj in range(count):
+                acc = bank("acc")
+                cols = slice(jj * P, (jj + 1) * P)
+                nc.tensor.matmul_mx(
+                    out=acc[:],
+                    lhsT=h_codes[:, cols].bitcast(E5M2), lhsT_scale=h_scales[:, cols],
+                    rhs=wt_codes[:].bitcast(E4M3), rhs_scale=wt_scales[:],
+                    start=True, stop=True,
+                )
+                nc.scalar.copy(out_sb[o][:, j0 + jj, :], acc[:])
+            nc.sync.dma_start(out_view[o, :, j0 : j0 + count, :], out_sb[o][:, j0 : j0 + count, :])
+
+        o_il = [keep.tile([P, D, PACK], BF16, name=f"o_il{o}", align_bytes=64) for o in range(HALVES)]
+        o_codes = [keep.tile([P, D], U32, name=f"o_codes{o}", align_bytes=64) for o in range(HALVES)]
+        o_scales = keep.tile([P, HALVES, D], U8, name="o_scales", align_bytes=64)
+
+        def round_out(o, a, cols, copy):
+            copy(
+                o_il[o][:, cols, 2 * a : 2 * a + 2].rearrange("p (c i) j -> p c j i", i=4),
+                out_sb[o][:, 2 * a : 2 * a + 2, cols].rearrange("p j (c i) -> p c j i", i=4),
+            )
+
+        def quantize_out(o, cols):
+            nc.vector.quantize_mx(
+                out=o_codes[o][:, cols].bitcast(E4M3), scales=o_scales[:, o, cols],
+                in_=o_il[o][:, cols, :].rearrange("p c j -> p (c j)"),
+            )
+
+        def store_codes(o):
+            nc.sync.dma_start(out_1[o].rearrange("p d l -> p (d l)").bitcast(I32), o_codes[o][:].bitcast(I32))
+
+        whole = slice(0, D)
+        deal_x(0, 0, nc.vector.tensor_copy)
+        deal_x(0, 1, nc.vector.tensor_copy)
+        score(0, 0, 0)
+        score(0, 0, 1)
+
+        w_words = w_il[:].rearrange("p c t -> p (c t)").bitcast(F32)
+        wt_il = keep.tile([P, D, PACK], BF16, name="wt_il", align_bytes=64)
+        wt_il_view = wt_il[:].rearrange("s (p u e) r -> s u p e r", u=2, e=2)
+        for u in range(2):
+            turned = bank("acc")
+            for r in range(PACK):
+                nc.tensor.transpose(turned[:, r * P : (r + 1) * P], w_words[:, 2 * r * P + u : 2 * (r + 1) * P : 2], ident[:])
+            turned_view = turned[:].bitcast(BF16).rearrange("s (r p e) -> s p e r", r=PACK, e=2)
+            for g in range(2):
+                nc.scalar.copy(wt_il_view[:, u, 64 * g : 64 * g + 64], turned_view[:, 64 * g : 64 * g + 64])
+
+        score(0, 1, 0)
+        wt_codes, wt_scales = quantize("wtq", wt_il[:], D, E4M3)
+        h00 = weigh(0, 0, 0, 2)
+        score(0, 1, 1)
+        back(0, 0, 2, h00)
+        deal_x(1, 0, nc.scalar.copy)
+        deal_x(1, 1, nc.scalar.copy)
+        back(0, 2, 2, weigh(0, 1, 0, 2))
+        score(1, 0, 0)
+        score(1, 0, 1)
+        score(1, 1, 0)
+        h10 = weigh(1, 0, 0, 2)
+        score(1, 1, 1)
+        back(1, 0, 2, h10)
+        h12 = weigh(1, 1, 0, 1)
+        h13 = weigh(1, 1, 1, 1)
+        back(1, 2, 1, h12)
+        back(1, 3, 1, h13)
+        round_out(0, 0, whole, nc.scalar.copy)
+        round_out(0, 1, whole, nc.vector.tensor_copy)
+        quantize_out(0, whole)
+        store_codes(0)
+        round_out(1, 0, whole, nc.vector.tensor_copy)
+        for g in range(2):
+            round_out(1, 1, slice(g * D // 2, (g + 1) * D // 2), nc.vector.tensor_copy)
+        for g in range(2):
+            quantize_out(1, slice(g * D // 2, (g + 1) * D // 2))
+        store_codes(1)
+        for q in range(4):
+            queue = nc.scalar if q % 2 else nc.sync
+            queue.dma_start(
+                out_2[:, 4 * q : 4 * q + 4, :].rearrange("o f d -> f o d").bitcast(I32),
+                o_scales[32 * q : 32 * q + 4, :, :].bitcast(I32),
+            )

@@ -28,11 +28,10 @@ def tile_attend_gnce_pl_x_ts_kernel(tc, xT, wT, y, wt, ts, offs, out_0, out_1, o
     nc = tc.nc
     with ExitStack() as ctx:
         keep = ctx.enter_context(tc.tile_pool(name="keep", bufs=1))
-        ring = ctx.enter_context(tc.tile_pool(name="ring", bufs=3))
         psum = ctx.enter_context(tc.psum_pool(name="psum", bufs=1))
 
-        def bank(tag):
-            return psum.tile([P, HALF], F32, name=tag, tag=tag, bufs={"sc": 3, "yt": 3, "acc": 2}[tag])
+        def bank(index):
+            return psum.tile([P, HALF], F32, name=f"bank{index}", tag=f"bank{index}")
 
         offsets = keep.tile([P, N // 16], U16, name="offsets")
         nc.sync.dma_start(offsets[:], offs)
@@ -56,12 +55,12 @@ def tile_attend_gnce_pl_x_ts_kernel(tc, xT, wT, y, wt, ts, offs, out_0, out_1, o
             for c in range(pieces):
                 cols = slice(c * T // pieces, (c + 1) * T // pieces)
                 nc.sync.dma_start(w_raw[t][:, cols], w_view[:, t, cols])
+        nc.sync.dma_start(y_raw[0][0][:], y_view[0, :, 0:2, :])
         nc.sync.dma_start(x_raw[0][:], x_view[:, :, 0:HALF])
-        for a in range(2):
-            nc.sync.dma_start(y_raw[0][a][:], y_view[0, :, 2 * a : 2 * a + 2, :])
+        nc.sync.dma_start(y_raw[0][1][:], y_view[0, :, 2:4, :])
+        nc.sync.dma_start(y_raw[1][0][:], y_view[1, :, 0:2, :])
         nc.sync.dma_start(x_raw[1][:], x_view[:, :, HALF:R])
-        for a in range(2):
-            nc.sync.dma_start(y_raw[1][a][:], y_view[1, :, 2 * a : 2 * a + 2, :])
+        nc.sync.dma_start(y_raw[1][1][:], y_view[1, :, 2:4, :])
 
         ident = keep.tile([P, P], F32, name="ident")
         make_identity(nc, ident[:])
@@ -70,7 +69,7 @@ def tile_attend_gnce_pl_x_ts_kernel(tc, xT, wT, y, wt, ts, offs, out_0, out_1, o
 
         ts_listed = keep.tile([P, N], F32, name="ts_listed")
         nc.vector.tensor_copy(ts_listed[:], ts_row[:].indirect(offsets[:]))
-        ts_bank = bank("sc")
+        ts_bank = bank(4)
         for t in range(PACK):
             nc.tensor.transpose(ts_bank[:, t * P : (t + 1) * P], ts_listed[:, t:N:PACK], ident[:])
         ts_col = keep.tile([P, PACK], F32, name="ts_col")
@@ -78,14 +77,14 @@ def tile_attend_gnce_pl_x_ts_kernel(tc, xT, wT, y, wt, ts, offs, out_0, out_1, o
 
         tw = [keep.tile([P, PACK, HALF], F32, name=f"tw{o}") for o in range(HALVES)]
         for o in range(HALVES):
-            wt_bank = bank("acc")
+            wt_bank = bank(6 + o)
             for j in range(PACK):
                 nc.tensor.transpose(wt_bank[:, j * P : (j + 1) * P], wt_sb[o][:, j : j + 1].to_broadcast([P, P]), ident[:])
             for t in range(PACK):
                 nc.scalar.activation(tw[o][:, t, :], wt_bank[:], ACT.Copy, scale=ts_col[:, t : t + 1])
 
-        def quantize(name, src, width, fmt):
-            codes = keep.tile([P, width], U32, name=name + "_codes", align_bytes=64)
+        def quantize(name, src, width, fmt, place=None):
+            codes = keep.tile([P, width], U32, name=name + "_codes", tag=place or name + "_codes", align_bytes=64)
             scales = keep.tile([P, width], U8, name=name + "_scales", align_bytes=64)
             nc.vector.quantize_mx(out=codes[:].bitcast(fmt), scales=scales[:], in_=src.rearrange("p c t -> p (c t)"))
             return codes, scales
@@ -94,29 +93,57 @@ def tile_attend_gnce_pl_x_ts_kernel(tc, xT, wT, y, wt, ts, offs, out_0, out_1, o
         xq = {}
 
         def deal_x(o, a, copy):
-            x_il[o, a] = keep.tile([P, PAIR, PACK], BF16, name=f"x_il{o}{a}", align_bytes=64)
+            x_il[o, a] = keep.tile([P, PAIR, PACK], BF16, name=f"x_il{o}{a}", tag=f"x_il{o}{a}", align_bytes=64)
             copy(
                 x_il[o, a][:].rearrange("p (j s) t -> p s t j", j=2),
                 x_raw[o][:].rearrange("p t (s j) -> p s t j", j=PACK)[:, :, :, 2 * a : 2 * a + 2],
             )
+
+        def quantize_x(o, a):
             xq[o, a] = quantize(f"xq{o}{a}", x_il[o, a][:], PAIR, E4M3)
 
         w_il = keep.tile([P, N, PACK], BF16, name="w_il", align_bytes=64)
-        w_dealt = w_il[:].rearrange("p (r s) t -> p t s r", r=PACK)
-        for t in range(PACK):
-            nc.vector.tensor_copy(w_dealt[:, t], w_raw[t][:].indirect(offsets[:]))
+        w_dealt = w_il[:].rearrange("p (r s) t -> p s t r", r=PACK)
+        wt_il = keep.tile([P, D, PACK], BF16, name="wt_il", align_bytes=64)
+        wt_words = wt_il[:].rearrange("s d r -> s (d r)").bitcast(F32).rearrange("s (p t v) -> s p t v", t=PACK, v=2)
+        for u in range(2):
+            listed = keep.tile([P, 2, N], BF16, name=f"listed{u}")
+            for tt in range(2):
+                nc.vector.tensor_copy(listed[:, tt, :], w_raw[2 * u + tt][:].indirect(offsets[:]))
+            nc.vector.tensor_copy(w_dealt[:, :, 2 * u : 2 * u + 2, :], listed[:].rearrange("p t (s r) -> p s t r", r=PACK))
+            turned = bank(2 + u)
+            for tt in range(2):
+                words = listed[:, tt, :].bitcast(F32)
+                for v in range(2):
+                    col = (2 * tt + v) * P
+                    nc.tensor.transpose(turned[:, col : col + P], words[:, v : N // 2 : 2], ident[:])
+            nc.scalar.copy(wt_words[:, :, 2 * u : 2 * u + 2, :], turned[:].rearrange("s (t v p) -> s p t v", t=2, v=2))
         wq_codes, wq_scales = quantize("wq", w_il[:], N, E4M3)
 
         diff = {}
+        y_dealt = {}
+
+        def deal_y(o, a, copy):
+            y_dealt[o, a] = keep.tile([P, 2, PACK, P], F32, name=f"y_dealt{o}{a}")
+            copy(y_dealt[o, a][:].rearrange("p j t s -> p j s t"), y_raw[o][a][:].rearrange("p j (s t) -> p j s t", t=PACK))
+
+        y_turned = {}
+
+        def turn_y(o, a):
+            for b in range(2):
+                yt = y_turned[o, a, b] = bank(4 + 2 * a + b)
+                for tt in range(2):
+                    for jj in range(2):
+                        col = (2 * tt + jj) * P
+                        t = 2 * b + tt
+                        rows = y_dealt[o, a][:, jj, t, :] if (o, a) in y_dealt else y_raw[o][a][:, jj, t:N:PACK]
+                        nc.tensor.transpose(yt[:, col : col + P], rows, ident[:])
+
+        sigs = {}
 
         def score(o, a, b):
-            yt = bank("yt")
-            for tt in range(2):
-                for jj in range(2):
-                    col = (2 * tt + jj) * P
-                    nc.tensor.transpose(yt[:, col : col + P], y_raw[o][a][:, jj, 2 * b + tt : N : PACK], ident[:])
-            sc = bank("sc")
-            sig = ring.tile([P, HALF], F32, name="sig", tag="sig")
+            sc = bank(b)
+            sig = keep.tile([P, HALF], F32, name=f"sig{o}{a}{b}")
             x_codes, x_scales = xq[o, a]
             for tt in range(2):
                 t = 2 * b + tt
@@ -132,12 +159,19 @@ def tile_attend_gnce_pl_x_ts_kernel(tc, xT, wT, y, wt, ts, offs, out_0, out_1, o
                 t = 2 * b + tt
                 cols = slice(tt * PAIR, (tt + 1) * PAIR)
                 nc.scalar.activation(sig[:, cols], sc[:, cols], ACT.Sigmoid, scale=ts_col[:, t : t + 1])
-            if b == 0:
-                diff[o, a] = ring.tile([P, PACK, PAIR], F32, name="diff", tag="diff")
-            nc.vector.tensor_tensor(diff[o, a][:, 2 * b : 2 * b + 2, :].rearrange("p t c -> p (t c)"), sig[:], yt[:], ALU.subtract)
+            sigs[o, a, b] = sig
+
+        def unit(o, a):
+            for b in range(2):
+                score(o, a, b)
+            diff[o, a] = keep.tile([P, PACK, PAIR], F32, name=f"diff{o}{a}")
+            for b in range(2):
+                nc.vector.tensor_tensor(
+                    diff[o, a][:, 2 * b : 2 * b + 2, :].rearrange("p t c -> p (t c)"), sigs[o, a, b][:], y_turned[o, a, b][:], ALU.subtract
+                )
 
         def weigh(o, a, first, count):
-            h_il = ring.tile([P, count * P, PACK], BF16, name="h_il", tag="h_il", align_bytes=64)
+            h_il = keep.tile([P, count * P, PACK], BF16, name=f"h_il{o}{a}{first}", align_bytes=64)
             cols = slice(first * P, (first + count) * P)
             nc.vector.tensor_tensor(
                 h_il[:].rearrange("p (c i) t -> p c t i", i=4),
@@ -150,10 +184,13 @@ def tile_attend_gnce_pl_x_ts_kernel(tc, xT, wT, y, wt, ts, offs, out_0, out_1, o
         out_sb = [keep.tile([P, PACK, D], F32, name=f"out_sb{o}") for o in range(HALVES)]
         out_view = out_0[0].rearrange("(o p j) d -> o p j d", o=HALVES, j=PACK)
 
-        def back(o, j0, count, h_il):
-            h_codes, h_scales = quantize(f"hq{o}{j0}", h_il[:], count * P, E5M2)
+        def quantize_h(o, j0, count, h_il):
+            return quantize(f"hq{o}{j0}", h_il[:], count * P, E5M2)
+
+        def back(o, j0, count, hq):
+            h_codes, h_scales = hq
             for jj in range(count):
-                acc = bank("acc")
+                acc = bank(2 + (j0 + jj) % 2)
                 cols = slice(jj * P, (jj + 1) * P)
                 nc.tensor.matmul_mx(
                     out=acc[:],
@@ -184,40 +221,36 @@ def tile_attend_gnce_pl_x_ts_kernel(tc, xT, wT, y, wt, ts, offs, out_0, out_1, o
             nc.sync.dma_start(out_1[o].rearrange("p d l -> p (d l)").bitcast(I32), o_codes[o][:].bitcast(I32))
 
         whole = slice(0, D)
+        turn_y(0, 0)
         deal_x(0, 0, nc.vector.tensor_copy)
-        deal_x(0, 1, nc.vector.tensor_copy)
-        score(0, 0, 0)
-        score(0, 0, 1)
-
-        w_words = w_il[:].rearrange("p c t -> p (c t)").bitcast(F32)
-        wt_il = keep.tile([P, D, PACK], BF16, name="wt_il", align_bytes=64)
-        wt_il_view = wt_il[:].rearrange("s (p u e) r -> s u p e r", u=2, e=2)
-        for u in range(2):
-            turned = bank("acc")
-            for r in range(PACK):
-                nc.tensor.transpose(turned[:, r * P : (r + 1) * P], w_words[:, 2 * r * P + u : 2 * (r + 1) * P : 2], ident[:])
-            turned_view = turned[:].bitcast(BF16).rearrange("s (r p e) -> s p e r", r=PACK, e=2)
-            for g in range(2):
-                nc.scalar.copy(wt_il_view[:, u, 64 * g : 64 * g + 64], turned_view[:, 64 * g : 64 * g + 64])
-
-        score(0, 1, 0)
-        wt_codes, wt_scales = quantize("wtq", wt_il[:], D, E4M3)
-        h00 = weigh(0, 0, 0, 2)
-        score(0, 1, 1)
-        back(0, 0, 2, h00)
+        quantize_x(0, 0)
+        deal_y(0, 1, nc.vector.tensor_copy)
+        deal_x(0, 1, nc.scalar.copy)
+        wt_codes, wt_scales = quantize("wtq", wt_il[:], D, E4M3, place="x_il00")
+        quantize_x(0, 1)
+        unit(0, 0)
+        turn_y(0, 1)
         deal_x(1, 0, nc.scalar.copy)
+        h00 = weigh(0, 0, 0, 2)
+        quantize_x(1, 0)
         deal_x(1, 1, nc.scalar.copy)
-        back(0, 2, 2, weigh(0, 1, 0, 2))
-        score(1, 0, 0)
-        score(1, 0, 1)
-        score(1, 1, 0)
-        h10 = weigh(1, 0, 0, 2)
-        score(1, 1, 1)
-        back(1, 0, 2, h10)
+        quantize_x(1, 1)
+        q00 = quantize_h(0, 0, 2, h00)
+        deal_y(1, 1, nc.vector.tensor_copy)
+        unit(0, 1)
+        turn_y(1, 0)
+        unit(1, 0)
+        q02 = quantize_h(0, 2, 2, weigh(0, 1, 0, 2))
+        back(0, 0, 2, q00)
+        turn_y(1, 1)
+        q10 = quantize_h(1, 0, 2, weigh(1, 0, 0, 2))
+        back(0, 2, 2, q02)
+        unit(1, 1)
+        back(1, 0, 2, q10)
         h12 = weigh(1, 1, 0, 1)
         h13 = weigh(1, 1, 1, 1)
-        back(1, 2, 1, h12)
-        back(1, 3, 1, h13)
+        back(1, 2, 1, quantize_h(1, 2, 1, h12))
+        back(1, 3, 1, quantize_h(1, 3, 1, h13))
         round_out(0, 0, whole, nc.scalar.copy)
         round_out(0, 1, whole, nc.vector.tensor_copy)
         quantize_out(0, whole)

@@ -41,7 +41,7 @@ def tile_attend_gnce_pl_x_ts_kernel(tc, xT, wT, y, wt, ts, offs, out_0, out_1, o
         y_view = y[0].rearrange("(o p j) i -> o p j i", o=HALVES, j=PACK)
         x_raw = [keep.tile([P, PACK, HALF], F32, name=f"x_raw{o}") for o in range(HALVES)]
         w_raw = [keep.tile([P, T], F32, name=f"w_raw{t}") for t in range(PACK)]
-        y_raw = [[keep.tile([P, 2, N], F32, name=f"y_raw{o}{a}") for a in range(2)] for o in range(HALVES)]
+        y_raw = [[keep.tile([P, 2, N], F32, name=f"y_raw{o}{a}", tag=f"y_raw{o}{a}") for a in range(2)] for o in range(HALVES)]
 
         ts_row = keep.tile([P, T], F32, name="ts_row")
         nc.vector.memset(ts_row[:], 0.0)
@@ -49,42 +49,23 @@ def tile_attend_gnce_pl_x_ts_kernel(tc, xT, wT, y, wt, ts, offs, out_0, out_1, o
         wt_sb = [keep.tile([P, PACK], F32, name=f"wt_sb{o}") for o in range(HALVES)]
         for o in range(HALVES):
             nc.scalar.dma_start(wt_sb[o][:], wt_view[o])
-        nc.scalar.dma_start(ts_row[0:1, :], ts[0:1, :])
-
-        for t, pieces in enumerate((4, 2, 1, 1)):
-            for c in range(pieces):
-                cols = slice(c * T // pieces, (c + 1) * T // pieces)
-                nc.sync.dma_start(w_raw[t][:, cols], w_view[:, t, cols])
-        nc.sync.dma_start(y_raw[0][0][:], y_view[0, :, 0:2, :])
         nc.sync.dma_start(x_raw[0][:], x_view[:, :, 0:HALF])
-        nc.sync.dma_start(y_raw[0][1][:], y_view[0, :, 2:4, :])
-        nc.sync.dma_start(y_raw[1][0][:], y_view[1, :, 0:2, :])
+        nc.sync.dma_start(ts_row[0:1, :], ts[0:1, :])
+        for t in range(PACK):
+            nc.sync.dma_start(w_raw[t][:], w_view[:, t, :])
+        for a in range(2):
+            nc.sync.dma_start(y_raw[0][a][:], y_view[0, :, 2 * a : 2 * a + 2, :])
         nc.sync.dma_start(x_raw[1][:], x_view[:, :, HALF:R])
-        nc.sync.dma_start(y_raw[1][1][:], y_view[1, :, 2:4, :])
+        for a in range(2):
+            nc.sync.dma_start(y_raw[1][a][:], y_view[1, :, 2 * a : 2 * a + 2, :])
 
         ident = keep.tile([P, P], F32, name="ident")
         make_identity(nc, ident[:])
         warm = keep.tile([P, 1], F32, name="warm")
         nc.scalar.activation(warm[:], ident[:, 0:1], ACT.Sigmoid)
 
-        ts_listed = keep.tile([P, N], F32, name="ts_listed")
-        nc.vector.tensor_copy(ts_listed[:], ts_row[:].indirect(offsets[:]))
-        ts_bank = bank(4)
-        for t in range(PACK):
-            nc.tensor.transpose(ts_bank[:, t * P : (t + 1) * P], ts_listed[:, t:N:PACK], ident[:])
-        ts_col = keep.tile([P, PACK], F32, name="ts_col")
-        nc.scalar.copy(ts_col[:], ts_bank[:, 0:HALF:P])
-
-        tw = [keep.tile([P, PACK, HALF], F32, name=f"tw{o}") for o in range(HALVES)]
-        for o in range(HALVES):
-            wt_bank = bank(6 + o)
-            for j in range(PACK):
-                nc.tensor.transpose(wt_bank[:, j * P : (j + 1) * P], wt_sb[o][:, j : j + 1].to_broadcast([P, P]), ident[:])
-            for t in range(PACK):
-                nc.scalar.activation(tw[o][:, t, :], wt_bank[:], ACT.Copy, scale=ts_col[:, t : t + 1])
-
-        def quantize(name, src, width, fmt, place=None):
-            codes = keep.tile([P, width], U32, name=name + "_codes", tag=place or name + "_codes", align_bytes=64)
+        def quantize(name, src, width, fmt):
+            codes = keep.tile([P, width], U32, name=name + "_codes", align_bytes=64)
             scales = keep.tile([P, width], U8, name=name + "_scales", align_bytes=64)
             nc.vector.quantize_mx(out=codes[:].bitcast(fmt), scales=scales[:], in_=src.rearrange("p c t -> p (c t)"))
             return codes, scales
@@ -102,22 +83,47 @@ def tile_attend_gnce_pl_x_ts_kernel(tc, xT, wT, y, wt, ts, offs, out_0, out_1, o
         def quantize_x(o, a):
             xq[o, a] = quantize(f"xq{o}{a}", x_il[o, a][:], PAIR, E4M3)
 
-        w_il = keep.tile([P, N, PACK], BF16, name="w_il", align_bytes=64)
+        for a in range(2):
+            deal_x(0, a, nc.scalar.copy)
+            quantize_x(0, a)
+
+        ts_listed = keep.tile([P, N], F32, name="ts_listed")
+        nc.vector.tensor_copy(ts_listed[:], ts_row[:].indirect(offsets[:]))
+        ts_bank = bank(2)
+        for t in range(PACK):
+            nc.tensor.transpose(ts_bank[:, t * P : (t + 1) * P], ts_listed[:, t:N:PACK], ident[:])
+        ts_col = keep.tile([P, PACK], F32, name="ts_col")
+        nc.scalar.copy(ts_col[:], ts_bank[:, 0:HALF:P])
+
+        tw = [keep.tile([P, PACK, HALF], F32, name=f"tw{o}") for o in range(HALVES)]
+        for o in range(HALVES):
+            wt_bank = bank(o)
+            for j in range(PACK):
+                nc.tensor.transpose(wt_bank[:, j * P : (j + 1) * P], wt_sb[o][:, j : j + 1].to_broadcast([P, P]), ident[:])
+            for t in range(PACK):
+                nc.scalar.activation(tw[o][:, t, :], wt_bank[:], ACT.Copy, scale=ts_col[:, t : t + 1])
+
+        last = PACK - 1
+        w_il = keep.tile([P, N, PACK], BF16, name="w_il", tag="w_il", align_bytes=64)
         w_dealt = w_il[:].rearrange("p (r s) t -> p s t r", r=PACK)
         wt_il = keep.tile([P, D, PACK], BF16, name="wt_il", align_bytes=64)
         wt_words = wt_il[:].rearrange("s d r -> s (d r)").bitcast(F32).rearrange("s (p t v) -> s p t v", t=PACK, v=2)
-        for u in range(2):
-            listed = keep.tile([P, 2, N], BF16, name=f"listed{u}")
-            for tt in range(2):
-                nc.vector.tensor_copy(listed[:, tt, :], w_raw[2 * u + tt][:].indirect(offsets[:]))
-            nc.vector.tensor_copy(w_dealt[:, :, 2 * u : 2 * u + 2, :], listed[:].rearrange("p t (s r) -> p s t r", r=PACK))
-            turned = bank(2 + u)
-            for tt in range(2):
-                words = listed[:, tt, :].bitcast(F32)
+        listed = keep.tile([P, last, N], BF16, name="listed")
+        for t in range(last):
+            nc.vector.tensor_copy(listed[:, t, :], w_raw[t][:].indirect(offsets[:]))
+        nc.vector.tensor_copy(w_dealt[:, :, 0:last, :], listed[:].rearrange("p t (s r) -> p s t r", r=PACK))
+
+        def turn_w(u, planes):
+            turned = bank(6 + u)
+            for tt, plane in enumerate(planes):
+                words = plane.bitcast(F32)
                 for v in range(2):
                     col = (2 * tt + v) * P
                     nc.tensor.transpose(turned[:, col : col + P], words[:, v : N // 2 : 2], ident[:])
             nc.scalar.copy(wt_words[:, :, 2 * u : 2 * u + 2, :], turned[:].rearrange("s (t v p) -> s p t v", t=2, v=2))
+
+        turn_w(0, [listed[:, 0, :], listed[:, 1, :]])
+        nc.vector.tensor_copy(w_dealt[:, :, last, :], w_raw[last][:].indirect(offsets[:]))
         wq_codes, wq_scales = quantize("wq", w_il[:], N, E4M3)
 
         diff = {}
@@ -131,19 +137,18 @@ def tile_attend_gnce_pl_x_ts_kernel(tc, xT, wT, y, wt, ts, offs, out_0, out_1, o
 
         def turn_y(o, a):
             for b in range(2):
-                yt = y_turned[o, a, b] = bank(4 + 2 * a + b)
+                yt = y_turned[o, a, b] = bank(2 + 2 * a + b)
                 for tt in range(2):
                     for jj in range(2):
                         col = (2 * tt + jj) * P
                         t = 2 * b + tt
-                        rows = y_dealt[o, a][:, jj, t, :] if (o, a) in y_dealt else y_raw[o][a][:, jj, t:N:PACK]
+                        rows = y_dealt[o, a][:, jj, t, :]
                         nc.tensor.transpose(yt[:, col : col + P], rows, ident[:])
 
         sigs = {}
 
-        def score(o, a, b):
+        def score(o, a, b, sig):
             sc = bank(b)
-            sig = keep.tile([P, HALF], F32, name=f"sig{o}{a}{b}")
             x_codes, x_scales = xq[o, a]
             for tt in range(2):
                 t = 2 * b + tt
@@ -161,17 +166,20 @@ def tile_attend_gnce_pl_x_ts_kernel(tc, xT, wT, y, wt, ts, offs, out_0, out_1, o
                 nc.scalar.activation(sig[:, cols], sc[:, cols], ACT.Sigmoid, scale=ts_col[:, t : t + 1])
             sigs[o, a, b] = sig
 
-        def unit(o, a):
+        def scores(o, a):
+            both = keep.tile([P, 2, HALF], F32, name=f"sig{o}{a}", tag="y_raw00" if (o, a) == (0, 0) else f"sig{o}{a}")
             for b in range(2):
-                score(o, a, b)
+                score(o, a, b, both[:, b, :])
+
+        def subtract(o, a):
             diff[o, a] = keep.tile([P, PACK, PAIR], F32, name=f"diff{o}{a}")
             for b in range(2):
                 nc.vector.tensor_tensor(
-                    diff[o, a][:, 2 * b : 2 * b + 2, :].rearrange("p t c -> p (t c)"), sigs[o, a, b][:], y_turned[o, a, b][:], ALU.subtract
+                    diff[o, a][:, 2 * b : 2 * b + 2, :].rearrange("p t c -> p (t c)"), sigs[o, a, b], y_turned[o, a, b][:], ALU.subtract
                 )
 
         def weigh(o, a, first, count):
-            h_il = keep.tile([P, count * P, PACK], BF16, name=f"h_il{o}{a}{first}", align_bytes=64)
+            h_il = keep.tile([P, count * P, PACK], BF16, name=f"h_il{o}{a}{first}", tag=f"h_il{o}{a}{first}", align_bytes=64)
             cols = slice(first * P, (first + count) * P)
             nc.vector.tensor_tensor(
                 h_il[:].rearrange("p (c i) t -> p c t i", i=4),
@@ -187,10 +195,10 @@ def tile_attend_gnce_pl_x_ts_kernel(tc, xT, wT, y, wt, ts, offs, out_0, out_1, o
         def quantize_h(o, j0, count, h_il):
             return quantize(f"hq{o}{j0}", h_il[:], count * P, E5M2)
 
-        def back(o, j0, count, hq):
+        def back(o, j0, count, hq, banks=6):
             h_codes, h_scales = hq
             for jj in range(count):
-                acc = bank(2 + (j0 + jj) % 2)
+                acc = bank(banks + (j0 + jj) % 2)
                 cols = slice(jj * P, (jj + 1) * P)
                 nc.tensor.matmul_mx(
                     out=acc[:],
@@ -201,14 +209,14 @@ def tile_attend_gnce_pl_x_ts_kernel(tc, xT, wT, y, wt, ts, offs, out_0, out_1, o
                 nc.scalar.copy(out_sb[o][:, j0 + jj, :], acc[:])
             nc.sync.dma_start(out_view[o, :, j0 : j0 + count, :], out_sb[o][:, j0 : j0 + count, :])
 
-        o_il = [keep.tile([P, D, PACK], BF16, name=f"o_il{o}", align_bytes=64) for o in range(HALVES)]
+        o_il = {}
         o_codes = [keep.tile([P, D], U32, name=f"o_codes{o}", align_bytes=64) for o in range(HALVES)]
         o_scales = keep.tile([P, HALVES, D], U8, name="o_scales", align_bytes=64)
 
-        def round_out(o, a, cols, copy):
+        def round_out(o, cols, copy):
             copy(
-                o_il[o][:, cols, 2 * a : 2 * a + 2].rearrange("p (c i) j -> p c j i", i=4),
-                out_sb[o][:, 2 * a : 2 * a + 2, cols].rearrange("p j (c i) -> p c j i", i=4),
+                o_il[o][:, cols, :].rearrange("p (c i) j -> p c j i", i=4),
+                out_sb[o][:, :, cols].rearrange("p j (c i) -> p c j i", i=4),
             )
 
         def quantize_out(o, cols):
@@ -221,45 +229,54 @@ def tile_attend_gnce_pl_x_ts_kernel(tc, xT, wT, y, wt, ts, offs, out_0, out_1, o
             nc.sync.dma_start(out_1[o].rearrange("p d l -> p (d l)").bitcast(I32), o_codes[o][:].bitcast(I32))
 
         whole = slice(0, D)
+        left, right = slice(0, D // 2), slice(D // 2, D)
+        deal_y(0, 0, nc.scalar.copy)
         turn_y(0, 0)
-        deal_x(0, 0, nc.vector.tensor_copy)
-        quantize_x(0, 0)
         deal_y(0, 1, nc.vector.tensor_copy)
-        deal_x(0, 1, nc.scalar.copy)
-        wt_codes, wt_scales = quantize("wtq", wt_il[:], D, E4M3, place="x_il00")
-        quantize_x(0, 1)
-        unit(0, 0)
         turn_y(0, 1)
-        deal_x(1, 0, nc.scalar.copy)
+        listed_last = keep.tile([P, N], BF16, name="listed_last", tag="y_raw01")
+        nc.vector.tensor_copy(listed_last[:], w_raw[last][:].indirect(offsets[:]))
+        scores(0, 0)
+        scores(0, 1)
+        subtract(0, 0)
+        turn_w(1, [listed[:, 2, :], listed_last[:]])
         h00 = weigh(0, 0, 0, 2)
+        deal_x(1, 0, nc.scalar.copy)
         quantize_x(1, 0)
-        deal_x(1, 1, nc.scalar.copy)
-        quantize_x(1, 1)
-        q00 = quantize_h(0, 0, 2, h00)
-        deal_y(1, 1, nc.vector.tensor_copy)
-        unit(0, 1)
+        deal_y(1, 0, nc.vector.tensor_copy)
         turn_y(1, 0)
-        unit(1, 0)
-        q02 = quantize_h(0, 2, 2, weigh(0, 1, 0, 2))
-        back(0, 0, 2, q00)
+        scores(1, 0)
+        deal_x(1, 1, nc.scalar.copy)
+        subtract(0, 1)
+        q00 = quantize_h(0, 0, 2, h00)
+        quantize_x(1, 1)
+        wt_codes, wt_scales = quantize("wtq", wt_il[:], D, E4M3)
+        h02 = weigh(0, 1, 0, 2)
+        deal_y(1, 1, nc.scalar.copy)
         turn_y(1, 1)
-        q10 = quantize_h(1, 0, 2, weigh(1, 0, 0, 2))
+        scores(1, 1)
+        back(0, 0, 2, q00)
+        subtract(1, 0)
+        q02 = quantize_h(0, 2, 2, h02)
+        h10 = weigh(1, 0, 0, 2)
         back(0, 2, 2, q02)
-        unit(1, 1)
-        back(1, 0, 2, q10)
+        subtract(1, 1)
+        back(1, 0, 2, quantize_h(1, 0, 2, h10))
         h12 = weigh(1, 1, 0, 1)
         h13 = weigh(1, 1, 1, 1)
-        back(1, 2, 1, quantize_h(1, 2, 1, h12))
-        back(1, 3, 1, quantize_h(1, 3, 1, h13))
-        round_out(0, 0, whole, nc.scalar.copy)
-        round_out(0, 1, whole, nc.vector.tensor_copy)
+        q12 = quantize_h(1, 2, 1, h12)
+        q13 = quantize_h(1, 3, 1, h13)
+        back(1, 2, 1, q12, banks=0)
+        back(1, 3, 1, q13, banks=0)
+        o_il[0] = keep.tile([P, D, PACK], BF16, name="o_il0", tag="h_il111", align_bytes=64)
+        o_il[1] = keep.tile([P, D, PACK], BF16, name="o_il1", align_bytes=64)
+        round_out(0, whole, nc.vector.tensor_copy)
         quantize_out(0, whole)
         store_codes(0)
-        round_out(1, 0, whole, nc.vector.tensor_copy)
-        for g in range(2):
-            round_out(1, 1, slice(g * D // 2, (g + 1) * D // 2), nc.vector.tensor_copy)
-        for g in range(2):
-            quantize_out(1, slice(g * D // 2, (g + 1) * D // 2))
+        round_out(1, left, nc.vector.tensor_copy)
+        round_out(1, right, nc.scalar.copy)
+        quantize_out(1, left)
+        quantize_out(1, right)
         store_codes(1)
         for q in range(4):
             queue = nc.scalar if q % 2 else nc.sync

@@ -49,12 +49,13 @@ def tile_attend_gnce_pl_x_ts_kernel(tc, xT, wT, y, wt, ts, offs, out_0, out_1, o
         wt_sb = [keep.tile([P, PACK], F32, name=f"wt_sb{o}") for o in range(HALVES)]
         for o in range(HALVES):
             nc.scalar.dma_start(wt_sb[o][:], wt_view[o])
-        nc.sync.dma_start(x_raw[0][:], x_view[:, :, 0:HALF])
+        nc.sync.dma_start(w_raw[0][:], w_view[:, 0, :])
         nc.sync.dma_start(ts_row[0:1, :], ts[0:1, :])
-        for t in range(PACK):
+        for t in range(1, PACK):
             nc.sync.dma_start(w_raw[t][:], w_view[:, t, :])
-        for a in range(2):
-            nc.sync.dma_start(y_raw[0][a][:], y_view[0, :, 2 * a : 2 * a + 2, :])
+        nc.sync.dma_start(y_raw[0][0][:], y_view[0, :, 0:2, :])
+        nc.sync.dma_start(x_raw[0][:], x_view[:, :, 0:HALF])
+        nc.sync.dma_start(y_raw[0][1][:], y_view[0, :, 2:4, :])
         nc.sync.dma_start(x_raw[1][:], x_view[:, :, HALF:R])
         for a in range(2):
             nc.sync.dma_start(y_raw[1][a][:], y_view[1, :, 2 * a : 2 * a + 2, :])
@@ -64,8 +65,8 @@ def tile_attend_gnce_pl_x_ts_kernel(tc, xT, wT, y, wt, ts, offs, out_0, out_1, o
         warm = keep.tile([P, 1], F32, name="warm")
         nc.scalar.activation(warm[:], ident[:, 0:1], ACT.Sigmoid)
 
-        def quantize(name, src, width, fmt):
-            codes = keep.tile([P, width], U32, name=name + "_codes", align_bytes=64)
+        def quantize(name, src, width, fmt, place=None):
+            codes = keep.tile([P, width], U32, name=name + "_codes", tag=place or name + "_codes", align_bytes=64)
             scales = keep.tile([P, width], U8, name=name + "_scales", align_bytes=64)
             nc.vector.quantize_mx(out=codes[:].bitcast(fmt), scales=scales[:], in_=src.rearrange("p c t -> p (c t)"))
             return codes, scales
@@ -83,10 +84,6 @@ def tile_attend_gnce_pl_x_ts_kernel(tc, xT, wT, y, wt, ts, offs, out_0, out_1, o
         def quantize_x(o, a):
             xq[o, a] = quantize(f"xq{o}{a}", x_il[o, a][:], PAIR, E4M3)
 
-        for a in range(2):
-            deal_x(0, a, nc.scalar.copy)
-            quantize_x(0, a)
-
         ts_listed = keep.tile([P, N], F32, name="ts_listed")
         nc.vector.tensor_copy(ts_listed[:], ts_row[:].indirect(offsets[:]))
         ts_bank = bank(2)
@@ -103,27 +100,22 @@ def tile_attend_gnce_pl_x_ts_kernel(tc, xT, wT, y, wt, ts, offs, out_0, out_1, o
             for t in range(PACK):
                 nc.scalar.activation(tw[o][:, t, :], wt_bank[:], ACT.Copy, scale=ts_col[:, t : t + 1])
 
-        last = PACK - 1
-        w_il = keep.tile([P, N, PACK], BF16, name="w_il", tag="w_il", align_bytes=64)
+        w_il = keep.tile([P, N, PACK], BF16, name="w_il", align_bytes=64)
         w_dealt = w_il[:].rearrange("p (r s) t -> p s t r", r=PACK)
         wt_il = keep.tile([P, D, PACK], BF16, name="wt_il", align_bytes=64)
         wt_words = wt_il[:].rearrange("s d r -> s (d r)").bitcast(F32).rearrange("s (p t v) -> s p t v", t=PACK, v=2)
-        listed = keep.tile([P, last, N], BF16, name="listed")
-        for t in range(last):
-            nc.vector.tensor_copy(listed[:, t, :], w_raw[t][:].indirect(offsets[:]))
-        nc.vector.tensor_copy(w_dealt[:, :, 0:last, :], listed[:].rearrange("p t (s r) -> p s t r", r=PACK))
-
-        def turn_w(u, planes):
+        for u in range(2):
+            listed = keep.tile([P, 2, N], BF16, name=f"listed{u}")
+            for tt in range(2):
+                nc.vector.tensor_copy(listed[:, tt, :], w_raw[2 * u + tt][:].indirect(offsets[:]))
+            nc.vector.tensor_copy(w_dealt[:, :, 2 * u : 2 * u + 2, :], listed[:].rearrange("p t (s r) -> p s t r", r=PACK))
             turned = bank(6 + u)
-            for tt, plane in enumerate(planes):
-                words = plane.bitcast(F32)
+            for tt in range(2):
+                words = listed[:, tt, :].bitcast(F32)
                 for v in range(2):
                     col = (2 * tt + v) * P
                     nc.tensor.transpose(turned[:, col : col + P], words[:, v : N // 2 : 2], ident[:])
             nc.scalar.copy(wt_words[:, :, 2 * u : 2 * u + 2, :], turned[:].rearrange("s (t v p) -> s p t v", t=2, v=2))
-
-        turn_w(0, [listed[:, 0, :], listed[:, 1, :]])
-        nc.vector.tensor_copy(w_dealt[:, :, last, :], w_raw[last][:].indirect(offsets[:]))
         wq_codes, wq_scales = quantize("wq", w_il[:], N, E4M3)
 
         diff = {}
@@ -142,7 +134,7 @@ def tile_attend_gnce_pl_x_ts_kernel(tc, xT, wT, y, wt, ts, offs, out_0, out_1, o
                     for jj in range(2):
                         col = (2 * tt + jj) * P
                         t = 2 * b + tt
-                        rows = y_dealt[o, a][:, jj, t, :]
+                        rows = y_dealt[o, a][:, jj, t, :] if (o, a) in y_dealt else y_raw[o][a][:, jj, t:N:PACK]
                         nc.tensor.transpose(yt[:, col : col + P], rows, ident[:])
 
         sigs = {}
@@ -167,7 +159,7 @@ def tile_attend_gnce_pl_x_ts_kernel(tc, xT, wT, y, wt, ts, offs, out_0, out_1, o
             sigs[o, a, b] = sig
 
         def scores(o, a):
-            both = keep.tile([P, 2, HALF], F32, name=f"sig{o}{a}", tag="y_raw00" if (o, a) == (0, 0) else f"sig{o}{a}")
+            both = keep.tile([P, 2, HALF], F32, name=f"sig{o}{a}", tag="y_raw01" if (o, a) == (0, 0) else f"sig{o}{a}")
             for b in range(2):
                 score(o, a, b, both[:, b, :])
 
@@ -209,57 +201,56 @@ def tile_attend_gnce_pl_x_ts_kernel(tc, xT, wT, y, wt, ts, offs, out_0, out_1, o
                 nc.scalar.copy(out_sb[o][:, j0 + jj, :], acc[:])
             nc.sync.dma_start(out_view[o, :, j0 : j0 + count, :], out_sb[o][:, j0 : j0 + count, :])
 
-        o_il = {}
         o_codes = [keep.tile([P, D], U32, name=f"o_codes{o}", align_bytes=64) for o in range(HALVES)]
         o_scales = keep.tile([P, HALVES, D], U8, name="o_scales", align_bytes=64)
 
-        def round_out(o, cols, copy):
+        def round_out(o, first, count, copy, place=None):
+            name = f"o_il{o}_{first}"
+            o_il = keep.tile([P, count, PACK], BF16, name=name, tag=place or name, align_bytes=64)
             copy(
-                o_il[o][:, cols, :].rearrange("p (c i) j -> p c j i", i=4),
-                out_sb[o][:, :, cols].rearrange("p j (c i) -> p c j i", i=4),
+                o_il[:].rearrange("p (c i) j -> p c j i", i=4),
+                out_sb[o][:, :, first : first + count].rearrange("p j (c i) -> p c j i", i=4),
             )
+            return o_il
 
-        def quantize_out(o, cols):
-            nc.vector.quantize_mx(
-                out=o_codes[o][:, cols].bitcast(E4M3), scales=o_scales[:, o, cols],
-                in_=o_il[o][:, cols, :].rearrange("p c j -> p (c j)"),
-            )
+        def quantize_out(o, first, o_il):
+            cols = slice(first, first + o_il.shape[1])
+            nc.vector.quantize_mx(out=o_codes[o][:, cols].bitcast(E4M3), scales=o_scales[:, o, cols], in_=o_il.rearrange("p c j -> p (c j)"))
 
         def store_codes(o):
             nc.sync.dma_start(out_1[o].rearrange("p d l -> p (d l)").bitcast(I32), o_codes[o][:].bitcast(I32))
 
-        whole = slice(0, D)
-        left, right = slice(0, D // 2), slice(D // 2, D)
-        deal_y(0, 0, nc.scalar.copy)
         turn_y(0, 0)
-        deal_y(0, 1, nc.vector.tensor_copy)
-        turn_y(0, 1)
-        listed_last = keep.tile([P, N], BF16, name="listed_last", tag="y_raw01")
-        nc.vector.tensor_copy(listed_last[:], w_raw[last][:].indirect(offsets[:]))
+        deal_x(0, 0, nc.vector.tensor_copy)
+        quantize_x(0, 0)
+        deal_x(0, 1, nc.scalar.copy)
+        quantize_x(0, 1)
+        deal_y(0, 1, nc.scalar.copy)
+        wt_codes, wt_scales = quantize("wtq", wt_il[:], D, E4M3, place="x_il00")
         scores(0, 0)
         scores(0, 1)
+        turn_y(0, 1)
         subtract(0, 0)
-        turn_w(1, [listed[:, 2, :], listed_last[:]])
         h00 = weigh(0, 0, 0, 2)
         deal_x(1, 0, nc.scalar.copy)
         quantize_x(1, 0)
         deal_y(1, 0, nc.vector.tensor_copy)
-        turn_y(1, 0)
         scores(1, 0)
+        turn_y(1, 0)
         deal_x(1, 1, nc.scalar.copy)
         subtract(0, 1)
         q00 = quantize_h(0, 0, 2, h00)
         quantize_x(1, 1)
-        wt_codes, wt_scales = quantize("wtq", wt_il[:], D, E4M3)
         h02 = weigh(0, 1, 0, 2)
         deal_y(1, 1, nc.scalar.copy)
-        turn_y(1, 1)
         scores(1, 1)
+        turn_y(1, 1)
         back(0, 0, 2, q00)
         subtract(1, 0)
         q02 = quantize_h(0, 2, 2, h02)
         h10 = weigh(1, 0, 0, 2)
         back(0, 2, 2, q02)
+        early = round_out(0, 3 * P, P, nc.scalar.copy)
         subtract(1, 1)
         back(1, 0, 2, quantize_h(1, 0, 2, h10))
         h12 = weigh(1, 1, 0, 1)
@@ -268,15 +259,15 @@ def tile_attend_gnce_pl_x_ts_kernel(tc, xT, wT, y, wt, ts, offs, out_0, out_1, o
         q13 = quantize_h(1, 3, 1, h13)
         back(1, 2, 1, q12, banks=0)
         back(1, 3, 1, q13, banks=0)
-        o_il[0] = keep.tile([P, D, PACK], BF16, name="o_il0", tag="h_il111", align_bytes=64)
-        o_il[1] = keep.tile([P, D, PACK], BF16, name="o_il1", align_bytes=64)
-        round_out(0, whole, nc.vector.tensor_copy)
-        quantize_out(0, whole)
+        late = round_out(0, 0, 3 * P, nc.vector.tensor_copy, place="h_il111")
+        quantize_out(0, 3 * P, early[:])
+        quantize_out(0, 0, late[:, 0:PAIR, :])
+        quantize_out(0, PAIR, late[:, PAIR : 3 * P, :])
         store_codes(0)
-        round_out(1, left, nc.vector.tensor_copy)
-        round_out(1, right, nc.scalar.copy)
-        quantize_out(1, left)
-        quantize_out(1, right)
+        left = round_out(1, 0, PAIR, nc.vector.tensor_copy)
+        right = round_out(1, PAIR, PAIR, nc.scalar.copy)
+        quantize_out(1, 0, left[:])
+        quantize_out(1, PAIR, right[:])
         store_codes(1)
         for q in range(4):
             queue = nc.scalar if q % 2 else nc.sync

@@ -22,6 +22,7 @@ PACK = 4
 HALF = P * PACK
 HALVES = R // HALF
 PAIR = 2 * P
+W0_FIRST = 1536
 
 
 def tile_attend_gnce_pl_x_ts_kernel(tc, xT, wT, y, wt, ts, offs, out_0, out_1, out_2):
@@ -39,50 +40,61 @@ def tile_attend_gnce_pl_x_ts_kernel(tc, xT, wT, y, wt, ts, offs, out_0, out_1, o
         x_view = xT[0].rearrange("(p t) r -> p t r", t=PACK)
         w_view = wT.rearrange("(p t) c -> p t c", t=PACK)
         y_view = y[0].rearrange("(o p j) i -> o p j i", o=HALVES, j=PACK)
-        x_raw = [keep.tile([P, PACK, HALF], F32, name=f"x_raw{o}") for o in range(HALVES)]
+        x_raw = [keep.tile([P, PACK, HALF], F32, name=f"x_raw{o}", tag=f"x_raw{o}", align_bytes=64) for o in range(HALVES)]
         w_raw = [keep.tile([P, T], F32, name=f"w_raw{t}") for t in range(PACK)]
-        y_raw = [[keep.tile([P, 2, N], F32, name=f"y_raw{o}{a}", tag=f"y_raw{o}{a}") for a in range(2)] for o in range(HALVES)]
+        y_raw = [[keep.tile([P, 2, N], F32, name=f"y_raw{o}{a}", tag=f"y_raw{o}{a}", align_bytes=64) for a in range(2)] for o in range(HALVES)]
 
         ts_row = keep.tile([P, T], F32, name="ts_row")
         nc.vector.memset(ts_row[:], 0.0)
-        wt_view = wt[0].rearrange("(o p j) e -> o p (j e)", o=HALVES, j=PACK)
-        wt_sb = [keep.tile([P, PACK], F32, name=f"wt_sb{o}") for o in range(HALVES)]
-        for o in range(HALVES):
-            nc.scalar.dma_start(wt_sb[o][:], wt_view[o])
-        nc.sync.dma_start(w_raw[0][:], w_view[:, 0, :])
+        wt_sb = keep.tile([P, HALVES, PACK], F32, name="wt_sb")
+        nc.scalar.dma_start(wt_sb[:], wt[0].rearrange("(o p j) e -> p o (j e)", o=HALVES, j=PACK))
+        nc.sync.dma_start(w_raw[0][:, 0:W0_FIRST], w_view[:, 0, 0:W0_FIRST])
         nc.sync.dma_start(ts_row[0:1, :], ts[0:1, :])
+        nc.sync.dma_start(w_raw[0][:, W0_FIRST:T], w_view[:, 0, W0_FIRST:T])
         for t in range(1, PACK):
             nc.sync.dma_start(w_raw[t][:], w_view[:, t, :])
-        nc.sync.dma_start(y_raw[0][0][:], y_view[0, :, 0:2, :])
-        nc.sync.dma_start(x_raw[0][:], x_view[:, :, 0:HALF])
-        nc.sync.dma_start(y_raw[0][1][:], y_view[0, :, 2:4, :])
-        nc.sync.dma_start(x_raw[1][:], x_view[:, :, HALF:R])
-        for a in range(2):
-            nc.sync.dma_start(y_raw[1][a][:], y_view[1, :, 2 * a : 2 * a + 2, :])
+
+        def load_x(o):
+            nc.sync.dma_start(x_raw[o][:], x_view[:, :, o * HALF : (o + 1) * HALF])
+
+        def load_y(o, a):
+            nc.sync.dma_start(y_raw[o][a][:], y_view[o, :, 2 * a : 2 * a + 2, :])
+
+        load_x(0)
+        load_x(1)
+        load_y(0, 0)
+        load_y(0, 1)
+        load_y(1, 0)
+        load_y(1, 1)
 
         ident = keep.tile([P, P], F32, name="ident")
         make_identity(nc, ident[:])
         warm = keep.tile([P, 1], F32, name="warm")
         nc.scalar.activation(warm[:], ident[:, 0:1], ACT.Sigmoid)
 
-        def quantize(name, src, width, fmt, place=None):
+        def mx_tiles(name, width, place=None):
             codes = keep.tile([P, width], U32, name=name + "_codes", tag=place or name + "_codes", align_bytes=64)
             scales = keep.tile([P, width], U8, name=name + "_scales", align_bytes=64)
-            nc.vector.quantize_mx(out=codes[:].bitcast(fmt), scales=scales[:], in_=src.rearrange("p c t -> p (c t)"))
             return codes, scales
+
+        def quantize(planes, src, fmt, first, count):
+            codes, scales = planes
+            cols = slice(first, first + count)
+            nc.vector.quantize_mx(out=codes[:, cols].bitcast(fmt), scales=scales[:, cols], in_=src.rearrange("p c t -> p (c t)"))
 
         x_il = {}
         xq = {}
 
-        def deal_x(o, a, copy):
-            x_il[o, a] = keep.tile([P, PAIR, PACK], BF16, name=f"x_il{o}{a}", tag=f"x_il{o}{a}", align_bytes=64)
+        def deal_x(o, a, copy, place=None):
+            x_il[o, a] = keep.tile([P, PAIR, PACK], BF16, name=f"x_il{o}{a}", tag=place or f"x_il{o}{a}", align_bytes=64)
             copy(
                 x_il[o, a][:].rearrange("p (j s) t -> p s t j", j=2),
                 x_raw[o][:].rearrange("p t (s j) -> p s t j", j=PACK)[:, :, :, 2 * a : 2 * a + 2],
             )
 
         def quantize_x(o, a):
-            xq[o, a] = quantize(f"xq{o}{a}", x_il[o, a][:], PAIR, E4M3)
+            xq[o, a] = mx_tiles(f"xq{o}{a}", PAIR)
+            quantize(xq[o, a], x_il[o, a][:], E4M3, 0, PAIR)
 
         ts_listed = keep.tile([P, N], F32, name="ts_listed")
         nc.vector.tensor_copy(ts_listed[:], ts_row[:].indirect(offsets[:]))
@@ -96,182 +108,236 @@ def tile_attend_gnce_pl_x_ts_kernel(tc, xT, wT, y, wt, ts, offs, out_0, out_1, o
         for o in range(HALVES):
             wt_bank = bank(o)
             for j in range(PACK):
-                nc.tensor.transpose(wt_bank[:, j * P : (j + 1) * P], wt_sb[o][:, j : j + 1].to_broadcast([P, P]), ident[:])
+                nc.tensor.transpose(wt_bank[:, j * P : (j + 1) * P], wt_sb[:, o, j : j + 1].to_broadcast([P, P]), ident[:])
             for t in range(PACK):
                 nc.scalar.activation(tw[o][:, t, :], wt_bank[:], ACT.Copy, scale=ts_col[:, t : t + 1])
 
         w_il = keep.tile([P, N, PACK], BF16, name="w_il", align_bytes=64)
-        w_dealt = w_il[:].rearrange("p (r s) t -> p s t r", r=PACK)
-        wt_il = keep.tile([P, D, PACK], BF16, name="wt_il", align_bytes=64)
-        wt_words = wt_il[:].rearrange("s d r -> s (d r)").bitcast(F32).rearrange("s (p t v) -> s p t v", t=PACK, v=2)
-        for u in range(2):
-            listed = keep.tile([P, 2, N], BF16, name=f"listed{u}")
-            for tt in range(2):
-                nc.vector.tensor_copy(listed[:, tt, :], w_raw[2 * u + tt][:].indirect(offsets[:]))
-            nc.vector.tensor_copy(w_dealt[:, :, 2 * u : 2 * u + 2, :], listed[:].rearrange("p t (s r) -> p s t r", r=PACK))
-            turned = bank(6 + u)
-            for tt in range(2):
-                words = listed[:, tt, :].bitcast(F32)
-                for v in range(2):
-                    col = (2 * tt + v) * P
-                    nc.tensor.transpose(turned[:, col : col + P], words[:, v : N // 2 : 2], ident[:])
-            nc.scalar.copy(wt_words[:, :, 2 * u : 2 * u + 2, :], turned[:].rearrange("s (t v p) -> s p t v", t=2, v=2))
-        wq_codes, wq_scales = quantize("wq", w_il[:], N, E4M3)
+        w_dealt = w_il[:].rearrange("p (r s) t -> p s r t", r=PACK)
+        w_words = w_il[:].rearrange("p c t -> p (c t)").bitcast(F32)
+        wt_il = {}
+        wtq = []
+        wq = mx_tiles("wq", N)
 
-        diff = {}
+        def gather_w(t):
+            nc.vector.tensor_copy(w_dealt[:, :, :, t], w_raw[t][:].indirect(offsets[:]))
+
+        def turn_w(u, index, place=None):
+            turned = bank(index)
+            for r in range(PACK):
+                nc.tensor.transpose(turned[:, r * P : (r + 1) * P], w_words[:, r * PAIR + u : (r + 1) * PAIR : 2], ident[:])
+            wt_il[u] = keep.tile([P, PAIR, PACK], BF16, name=f"wt_il{u}", tag=place or f"wt_il{u}", align_bytes=64)
+            nc.scalar.copy(wt_il[u][:], turned[:].bitcast(BF16).rearrange("s (r c) -> s c r", r=PACK))
+
+        def quantize_w(first, count):
+            quantize(wq, w_il[:, first : first + count, :], E4M3, first, count)
+
+        def quantize_wt(u, place=None):
+            if not wtq:
+                wtq.extend(mx_tiles("wtq", D, place))
+            quantize(wtq, wt_il[u][:], E4M3, u * PAIR, PAIR)
+
         y_dealt = {}
 
-        def deal_y(o, a, copy):
-            y_dealt[o, a] = keep.tile([P, 2, PACK, P], F32, name=f"y_dealt{o}{a}")
+        def deal_y(o, a, copy, place=None):
+            y_dealt[o, a] = keep.tile([P, 2, PACK, P], F32, name=f"y_dealt{o}{a}", tag=place or f"y_dealt{o}{a}", align_bytes=64)
             copy(y_dealt[o, a][:].rearrange("p j t s -> p j s t"), y_raw[o][a][:].rearrange("p j (s t) -> p j s t", t=PACK))
 
         y_turned = {}
 
-        def turn_y(o, a):
-            for b in range(2):
-                yt = y_turned[o, a, b] = bank(2 + 2 * a + b)
-                for tt in range(2):
-                    for jj in range(2):
-                        col = (2 * tt + jj) * P
-                        t = 2 * b + tt
-                        rows = y_dealt[o, a][:, jj, t, :] if (o, a) in y_dealt else y_raw[o][a][:, jj, t:N:PACK]
-                        nc.tensor.transpose(yt[:, col : col + P], rows, ident[:])
+        def turn_y(o, j, index):
+            yt = y_turned[o, j] = bank(index)
+            a, jj = divmod(j, 2)
+            for t in range(PACK):
+                rows = y_dealt[o, a][:, jj, t, :] if (o, a) in y_dealt else y_raw[o][a][:, jj, t:N:PACK]
+                nc.tensor.transpose(yt[:, t * P : (t + 1) * P], rows, ident[:])
 
         sigs = {}
 
-        def score(o, a, b, sig):
-            sc = bank(b)
+        def scores(o, a, banks, place=None):
+            sig = sigs[o, a] = keep.tile([P, PACK, PAIR], F32, name=f"sig{o}{a}", tag=place or f"sig{o}{a}", align_bytes=64)
             x_codes, x_scales = xq[o, a]
-            for tt in range(2):
-                t = 2 * b + tt
-                slots = slice(t * P, (t + 1) * P)
-                cols = slice(tt * PAIR, (tt + 1) * PAIR)
-                nc.tensor.matmul_mx(
-                    out=sc[:, cols],
-                    lhsT=wq_codes[:, slots].bitcast(E4M3), lhsT_scale=wq_scales[:, slots],
-                    rhs=x_codes[:].bitcast(E4M3), rhs_scale=x_scales[:],
-                    start=True, stop=True,
-                )
-            for tt in range(2):
-                t = 2 * b + tt
-                cols = slice(tt * PAIR, (tt + 1) * PAIR)
-                nc.scalar.activation(sig[:, cols], sc[:, cols], ACT.Sigmoid, scale=ts_col[:, t : t + 1])
-            sigs[o, a, b] = sig
+            share = PACK // len(banks)
+            for b, index in enumerate(banks):
+                sc = bank(index)
+                for tt in range(share):
+                    slots = slice((share * b + tt) * P, (share * b + tt + 1) * P)
+                    nc.tensor.matmul_mx(
+                        out=sc[:, tt * PAIR : (tt + 1) * PAIR],
+                        lhsT=wq[0][:, slots].bitcast(E4M3), lhsT_scale=wq[1][:, slots],
+                        rhs=x_codes[:].bitcast(E4M3), rhs_scale=x_scales[:],
+                        start=True, stop=True,
+                    )
+                for tt in range(share):
+                    t = share * b + tt
+                    nc.scalar.activation(sig[:, t, :], sc[:, tt * PAIR : (tt + 1) * PAIR], ACT.Sigmoid, scale=ts_col[:, t : t + 1])
 
-        def scores(o, a):
-            both = keep.tile([P, 2, HALF], F32, name=f"sig{o}{a}", tag="y_raw01" if (o, a) == (0, 0) else f"sig{o}{a}")
-            for b in range(2):
-                score(o, a, b, both[:, b, :])
+        diff = {}
 
-        def subtract(o, a):
-            diff[o, a] = keep.tile([P, PACK, PAIR], F32, name=f"diff{o}{a}")
-            for b in range(2):
-                nc.vector.tensor_tensor(
-                    diff[o, a][:, 2 * b : 2 * b + 2, :].rearrange("p t c -> p (t c)"), sigs[o, a, b], y_turned[o, a, b][:], ALU.subtract
-                )
-
-        def weigh(o, a, first, count):
-            h_il = keep.tile([P, count * P, PACK], BF16, name=f"h_il{o}{a}{first}", tag=f"h_il{o}{a}{first}", align_bytes=64)
-            cols = slice(first * P, (first + count) * P)
+        def subtract(o, j, place=None):
+            diff[o, j] = keep.tile([P, PACK, P], F32, name=f"diff{o}{j}", tag=place or f"diff{o}{j}", align_bytes=64)
+            a, jj = divmod(j, 2)
             nc.vector.tensor_tensor(
-                h_il[:].rearrange("p (c i) t -> p c t i", i=4),
-                diff[o, a][:, :, cols].rearrange("p t (c i) -> p c t i", i=4),
-                tw[o][:, :, a * PAIR : (a + 1) * PAIR][:, :, cols].rearrange("p t (c i) -> p c t i", i=4),
+                diff[o, j][:], sigs[o, a][:, :, jj * P : (jj + 1) * P], y_turned[o, j][:].rearrange("p (t c) -> p t c", t=PACK), ALU.subtract
+            )
+
+        h_il = {}
+
+        def weigh(o, j):
+            a, jj = divmod(j, 2)
+            if jj == 0:
+                h_il[o, a] = keep.tile([P, PAIR, PACK], BF16, name=f"h_il{o}{a}", tag=f"h_il{o}{a}", align_bytes=64)
+            nc.vector.tensor_tensor(
+                h_il[o, a][:, jj * P : (jj + 1) * P, :].rearrange("p (c i) t -> p c t i", i=4),
+                diff[o, j][:].rearrange("p t (c i) -> p c t i", i=4),
+                tw[o][:, :, j * P : (j + 1) * P].rearrange("p t (c i) -> p c t i", i=4),
                 ALU.mult,
             )
-            return h_il
+
+        hq = [mx_tiles(f"hq{o}", HALF) for o in range(HALVES)]
+
+        def quantize_h(o, j, count):
+            a, jj = divmod(j, 2)
+            quantize(hq[o], h_il[o, a][:, jj * P : (jj + count) * P, :], E5M2, j * P, count * P)
 
         out_sb = [keep.tile([P, PACK, D], F32, name=f"out_sb{o}") for o in range(HALVES)]
         out_view = out_0[0].rearrange("(o p j) d -> o p j d", o=HALVES, j=PACK)
 
-        def quantize_h(o, j0, count, h_il):
-            return quantize(f"hq{o}{j0}", h_il[:], count * P, E5M2)
+        acc = {}
 
-        def back(o, j0, count, hq, banks=6):
-            h_codes, h_scales = hq
-            for jj in range(count):
-                acc = bank(banks + (j0 + jj) % 2)
-                cols = slice(jj * P, (jj + 1) * P)
-                nc.tensor.matmul_mx(
-                    out=acc[:],
-                    lhsT=h_codes[:, cols].bitcast(E5M2), lhsT_scale=h_scales[:, cols],
-                    rhs=wt_codes[:].bitcast(E4M3), rhs_scale=wt_scales[:],
-                    start=True, stop=True,
-                )
-                nc.scalar.copy(out_sb[o][:, j0 + jj, :], acc[:])
-            nc.sync.dma_start(out_view[o, :, j0 : j0 + count, :], out_sb[o][:, j0 : j0 + count, :])
+        def back(o, j, index):
+            acc[o, j] = bank(index)
+            cols = slice(j * P, (j + 1) * P)
+            nc.tensor.matmul_mx(
+                out=acc[o, j][:],
+                lhsT=hq[o][0][:, cols].bitcast(E5M2), lhsT_scale=hq[o][1][:, cols],
+                rhs=wtq[0][:].bitcast(E4M3), rhs_scale=wtq[1][:],
+                start=True, stop=True,
+            )
+
+        def empty(o, j, copy, first=0, count=D):
+            copy(
+                out_sb[o][:, j, first : first + count].rearrange("p (c u e) -> p c u e", u=2, e=2),
+                acc[o, j][:].rearrange("p (u c e) -> p c u e", u=2, e=2)[:, first // PACK : (first + count) // PACK],
+            )
+
+        def store_out(o, j, count):
+            nc.sync.dma_start(out_view[o, :, j : j + count, :], out_sb[o][:, j : j + count, :])
 
         o_codes = [keep.tile([P, D], U32, name=f"o_codes{o}", align_bytes=64) for o in range(HALVES)]
         o_scales = keep.tile([P, HALVES, D], U8, name="o_scales", align_bytes=64)
+        o_il = [keep.tile([P, D, PACK], BF16, name=f"o_il{o}", align_bytes=64) for o in range(HALVES)]
 
-        def round_out(o, first, count, copy, place=None):
-            name = f"o_il{o}_{first}"
-            o_il = keep.tile([P, count, PACK], BF16, name=name, tag=place or name, align_bytes=64)
+        def round_out(o, first, count, copy):
             copy(
-                o_il[:].rearrange("p (c i) j -> p c j i", i=4),
+                o_il[o][:, first : first + count, :].rearrange("p (c i) j -> p c j i", i=4),
                 out_sb[o][:, :, first : first + count].rearrange("p j (c i) -> p c j i", i=4),
             )
-            return o_il
 
-        def quantize_out(o, first, o_il):
-            cols = slice(first, first + o_il.shape[1])
-            nc.vector.quantize_mx(out=o_codes[o][:, cols].bitcast(E4M3), scales=o_scales[:, o, cols], in_=o_il.rearrange("p c j -> p (c j)"))
+        def quantize_out(o, first, count):
+            quantize((o_codes[o], o_scales[:, o, :]), o_il[o][:, first : first + count, :], E4M3, first, count)
 
-        def store_codes(o):
-            nc.sync.dma_start(out_1[o].rearrange("p d l -> p (d l)").bitcast(I32), o_codes[o][:].bitcast(I32))
-
-        turn_y(0, 0)
-        deal_x(0, 0, nc.vector.tensor_copy)
-        quantize_x(0, 0)
-        deal_x(0, 1, nc.scalar.copy)
-        quantize_x(0, 1)
-        deal_y(0, 1, nc.scalar.copy)
-        wt_codes, wt_scales = quantize("wtq", wt_il[:], D, E4M3, place="x_il00")
-        scores(0, 0)
-        scores(0, 1)
-        turn_y(0, 1)
-        subtract(0, 0)
-        h00 = weigh(0, 0, 0, 2)
-        deal_x(1, 0, nc.scalar.copy)
-        quantize_x(1, 0)
-        deal_y(1, 0, nc.vector.tensor_copy)
-        scores(1, 0)
-        turn_y(1, 0)
-        deal_x(1, 1, nc.scalar.copy)
-        subtract(0, 1)
-        q00 = quantize_h(0, 0, 2, h00)
-        quantize_x(1, 1)
-        h02 = weigh(0, 1, 0, 2)
-        deal_y(1, 1, nc.scalar.copy)
-        scores(1, 1)
-        turn_y(1, 1)
-        back(0, 0, 2, q00)
-        subtract(1, 0)
-        q02 = quantize_h(0, 2, 2, h02)
-        h10 = weigh(1, 0, 0, 2)
-        back(0, 2, 2, q02)
-        early = round_out(0, 3 * P, P, nc.scalar.copy)
-        subtract(1, 1)
-        back(1, 0, 2, quantize_h(1, 0, 2, h10))
-        h12 = weigh(1, 1, 0, 1)
-        h13 = weigh(1, 1, 1, 1)
-        q12 = quantize_h(1, 2, 1, h12)
-        q13 = quantize_h(1, 3, 1, h13)
-        back(1, 2, 1, q12, banks=0)
-        back(1, 3, 1, q13, banks=0)
-        late = round_out(0, 0, 3 * P, nc.vector.tensor_copy, place="h_il111")
-        quantize_out(0, 3 * P, early[:])
-        quantize_out(0, 0, late[:, 0:PAIR, :])
-        quantize_out(0, PAIR, late[:, PAIR : 3 * P, :])
-        store_codes(0)
-        left = round_out(1, 0, PAIR, nc.vector.tensor_copy)
-        right = round_out(1, PAIR, PAIR, nc.scalar.copy)
-        quantize_out(1, 0, left[:])
-        quantize_out(1, PAIR, right[:])
-        store_codes(1)
-        for q in range(4):
-            queue = nc.scalar if q % 2 else nc.sync
-            queue.dma_start(
-                out_2[:, 4 * q : 4 * q + 4, :].rearrange("o f d -> f o d").bitcast(I32),
-                o_scales[32 * q : 32 * q + 4, :, :].bitcast(I32),
+        def store_codes(o, first=0, count=D):
+            nc.sync.dma_start(
+                out_1[o].rearrange("p d l -> p (d l)").bitcast(I32)[:, first : first + count], o_codes[o][:, first : first + count].bitcast(I32)
             )
+
+        def store_scales():
+            for q in range(4):
+                queue = nc.scalar if q % 2 else nc.sync
+                queue.dma_start(
+                    out_2[:, 4 * q : 4 * q + 4, :].rearrange("o f d -> f o d").bitcast(I32),
+                    o_scales[32 * q : 32 * q + 4, :, :].bitcast(I32),
+                )
+
+        on_vector, on_scalar = nc.vector.tensor_copy, nc.scalar.copy
+
+        gather_w(0)
+        gather_w(1)
+        turn_w(0, 6)
+        gather_w(2)
+        gather_w(3)
+        quantize_w(0, PAIR)
+        quantize_w(PAIR, PAIR)
+        turn_w(1, 3)
+        deal_x(0, 0, on_vector)
+        deal_x(0, 1, on_vector)
+        quantize_x(0, 0)
+        quantize_x(0, 1)
+        scores(0, 0, (0, 1, 6, 7))
+        scores(0, 1, (4, 5))
+        deal_x(1, 0, on_vector)
+        quantize_wt(0, "x_il01")
+        quantize_x(1, 0)
+        deal_y(0, 0, on_vector)
+        turn_y(0, 0, 2)
+        turn_y(0, 1, 3)
+        deal_x(1, 1, on_vector, "y_raw00")
+        deal_y(0, 1, on_scalar)
+        scores(1, 0, (0, 1))
+        subtract(0, 0)
+        quantize_wt(1)
+        subtract(0, 1)
+        quantize_x(1, 1)
+        turn_y(0, 2, 4)
+        turn_y(0, 3, 5)
+        weigh(0, 0)
+        weigh(0, 1)
+        deal_y(1, 0, on_scalar)
+        deal_y(1, 1, on_scalar)
+        scores(1, 1, (0, 1))
+        subtract(0, 2)
+        quantize_h(0, 0, 2)
+        back(0, 0, 6)
+        back(0, 1, 7)
+        turn_y(1, 0, 2)
+        turn_y(1, 1, 3)
+        subtract(0, 3)
+        empty(0, 0, on_scalar)
+        empty(0, 1, on_scalar)
+        store_out(0, 0, 2)
+        weigh(0, 2)
+        weigh(0, 3)
+        turn_y(1, 2, 4)
+        turn_y(1, 3, 5)
+        subtract(1, 0)
+        quantize_h(0, 2, 2)
+        back(0, 2, 0)
+        back(0, 3, 1)
+        empty(0, 2, on_scalar)
+        empty(0, 3, on_scalar)
+        store_out(0, 2, 2)
+        subtract(1, 1)
+        weigh(1, 0)
+        weigh(1, 1)
+        subtract(1, 2)
+        quantize_h(1, 0, 2)
+        back(1, 0, 6)
+        back(1, 1, 7)
+        empty(1, 0, on_scalar)
+        empty(1, 1, on_scalar)
+        store_out(1, 0, 2)
+        round_out(0, 0, PAIR, on_scalar)
+        subtract(1, 3)
+        weigh(1, 2)
+        weigh(1, 3)
+        quantize_h(1, 2, 1)
+        quantize_h(1, 3, 1)
+        back(1, 2, 0)
+        back(1, 3, 1)
+        round_out(0, PAIR, PAIR, on_vector)
+        quantize_out(0, 0, PAIR)
+        quantize_out(0, PAIR, PAIR)
+        empty(1, 2, on_scalar)
+        store_codes(0)
+        store_out(1, 2, 1)
+        empty(1, 3, on_vector, 0, PAIR)
+        empty(1, 3, on_vector, PAIR, PAIR)
+        store_out(1, 3, 1)
+        round_out(1, 0, 160, on_scalar)
+        round_out(1, 160, 96, on_vector)
+        round_out(1, PAIR, PAIR, on_vector)
+        quantize_out(1, 0, PAIR)
+        quantize_out(1, PAIR, PAIR)
+        store_codes(1)
+        store_scales()

@@ -61,8 +61,8 @@ def tile_attend_gnce_pl_x_ts_kernel(tc, xT, wT, y, wt, ts, offs, out_0, out_1, o
             nc.sync.dma_start(y_raw[o][a][:], y_view[o, :, 2 * a : 2 * a + 2, :])
 
         load_x(0)
-        load_x(1)
         load_y(0, 0)
+        load_x(1)
         load_y(0, 1)
         load_y(1, 0)
         load_y(1, 1)
@@ -113,29 +113,34 @@ def tile_attend_gnce_pl_x_ts_kernel(tc, xT, wT, y, wt, ts, offs, out_0, out_1, o
                 nc.scalar.activation(tw[o][:, t, :], wt_bank[:], ACT.Copy, scale=ts_col[:, t : t + 1])
 
         w_il = keep.tile([P, N, PACK], BF16, name="w_il", align_bytes=64)
-        w_dealt = w_il[:].rearrange("p (r s) t -> p s r t", r=PACK)
-        w_words = w_il[:].rearrange("p c t -> p (c t)").bitcast(F32)
-        wt_il = {}
+        w_dealt = w_il[:].rearrange("p (r s) t -> p s t r", r=PACK)
+        listed = [keep.tile([P, 2, N], BF16, name=f"listed{u}") for u in range(2)]
+        wt_il = keep.tile([P, D, PACK], BF16, name="wt_il", align_bytes=64)
+        wt_words = wt_il[:].rearrange("s d r -> s (d r)").bitcast(F32).rearrange("s (p t v) -> s p t v", t=PACK, v=2)
         wtq = []
         wq = mx_tiles("wq", N)
 
         def gather_w(t):
-            nc.vector.tensor_copy(w_dealt[:, :, :, t], w_raw[t][:].indirect(offsets[:]))
+            nc.vector.tensor_copy(listed[t // 2][:, t % 2, :], w_raw[t][:].indirect(offsets[:]))
 
-        def turn_w(u, index, place=None):
+        def weave_w(u):
+            nc.vector.tensor_copy(w_dealt[:, :, 2 * u : 2 * u + 2, :], listed[u][:].rearrange("p t (s r) -> p s t r", r=PACK))
+
+        def turn_w(u, index):
             turned = bank(index)
-            for r in range(PACK):
-                nc.tensor.transpose(turned[:, r * P : (r + 1) * P], w_words[:, r * PAIR + u : (r + 1) * PAIR : 2], ident[:])
-            wt_il[u] = keep.tile([P, PAIR, PACK], BF16, name=f"wt_il{u}", tag=place or f"wt_il{u}", align_bytes=64)
-            nc.scalar.copy(wt_il[u][:], turned[:].bitcast(BF16).rearrange("s (r c) -> s c r", r=PACK))
+            for tt in range(2):
+                words = listed[u][:, tt, :].bitcast(F32)
+                for v in range(2):
+                    col = (2 * tt + v) * P
+                    nc.tensor.transpose(turned[:, col : col + P], words[:, v : N // 2 : 2], ident[:])
+            nc.scalar.copy(wt_words[:, :, 2 * u : 2 * u + 2, :], turned[:].rearrange("s (t v p) -> s p t v", t=2, v=2))
 
         def quantize_w(first, count):
             quantize(wq, w_il[:, first : first + count, :], E4M3, first, count)
 
-        def quantize_wt(u, place=None):
-            if not wtq:
-                wtq.extend(mx_tiles("wtq", D, place))
-            quantize(wtq, wt_il[u][:], E4M3, u * PAIR, PAIR)
+        def quantize_wt(place=None):
+            wtq.extend(mx_tiles("wtq", D, place))
+            quantize(wtq, wt_il[:], E4M3, 0, D)
 
         y_dealt = {}
 
@@ -154,8 +159,14 @@ def tile_attend_gnce_pl_x_ts_kernel(tc, xT, wT, y, wt, ts, offs, out_0, out_1, o
 
         sigs = {}
 
-        def scores(o, a, banks, place=None):
-            sig = sigs[o, a] = keep.tile([P, PACK, PAIR], F32, name=f"sig{o}{a}", tag=place or f"sig{o}{a}", align_bytes=64)
+        def sigmoids(o, first, count, place):
+            name = f"sig{o}{first}"
+            tile = keep.tile([P, count, PACK, PAIR], F32, name=name, tag=place or name, align_bytes=64)
+            for a in range(count):
+                sigs[o, first + a] = tile[:, a]
+
+        def scores(o, a, banks):
+            sig = sigs[o, a]
             x_codes, x_scales = xq[o, a]
             share = PACK // len(banks)
             for b, index in enumerate(banks):
@@ -175,67 +186,78 @@ def tile_attend_gnce_pl_x_ts_kernel(tc, xT, wT, y, wt, ts, offs, out_0, out_1, o
         diff = {}
 
         def subtract(o, j, place=None):
-            diff[o, j] = keep.tile([P, PACK, P], F32, name=f"diff{o}{j}", tag=place or f"diff{o}{j}", align_bytes=64)
             a, jj = divmod(j, 2)
+            if (o, a) not in diff:
+                diff[o, a] = keep.tile([P, PACK, PAIR], F32, name=f"diff{o}{a}", tag=place or f"diff{o}{a}", align_bytes=64)
+            cols = slice(jj * P, (jj + 1) * P)
             nc.vector.tensor_tensor(
-                diff[o, j][:], sigs[o, a][:, :, jj * P : (jj + 1) * P], y_turned[o, j][:].rearrange("p (t c) -> p t c", t=PACK), ALU.subtract
+                diff[o, a][:, :, cols], sigs[o, a][:, :, cols], y_turned[o, j][:].rearrange("p (t c) -> p t c", t=PACK), ALU.subtract
             )
 
         h_il = {}
 
-        def weigh(o, j):
+        def weigh(o, j, count=1, place=None):
             a, jj = divmod(j, 2)
-            if jj == 0:
-                h_il[o, a] = keep.tile([P, PAIR, PACK], BF16, name=f"h_il{o}{a}", tag=f"h_il{o}{a}", align_bytes=64)
+            if (o, a) not in h_il:
+                h_il[o, a] = keep.tile([P, PAIR, PACK], BF16, name=f"h_il{o}{a}", tag=place or f"h_il{o}{a}", align_bytes=64)
+            cols = slice(jj * P, (jj + count) * P)
             nc.vector.tensor_tensor(
-                h_il[o, a][:, jj * P : (jj + 1) * P, :].rearrange("p (c i) t -> p c t i", i=4),
-                diff[o, j][:].rearrange("p t (c i) -> p c t i", i=4),
-                tw[o][:, :, j * P : (j + 1) * P].rearrange("p t (c i) -> p c t i", i=4),
+                h_il[o, a][:, cols, :].rearrange("p (c i) t -> p c t i", i=4),
+                diff[o, a][:, :, cols].rearrange("p t (c i) -> p c t i", i=4),
+                tw[o][:, :, j * P : (j + count) * P].rearrange("p t (c i) -> p c t i", i=4),
                 ALU.mult,
             )
 
-        hq = [mx_tiles(f"hq{o}", HALF) for o in range(HALVES)]
+        hq = {}
 
-        def quantize_h(o, j, count):
+        def quantize_h(o, j, count, place=None):
             a, jj = divmod(j, 2)
-            quantize(hq[o], h_il[o, a][:, jj * P : (jj + count) * P, :], E5M2, j * P, count * P)
+            if (o, a) not in hq:
+                hq[o, a] = mx_tiles(f"hq{o}{a}", PAIR, place)
+            quantize(hq[o, a], h_il[o, a][:, jj * P : (jj + count) * P, :], E5M2, jj * P, count * P)
 
-        out_sb = [keep.tile([P, PACK, D], F32, name=f"out_sb{o}") for o in range(HALVES)]
+        out_sb = {}
+
+        def results(o, place=None):
+            out_sb[o] = keep.tile([P, PACK, D], F32, name=f"out_sb{o}", tag=place or f"out_sb{o}", align_bytes=64)
+
         out_view = out_0[0].rearrange("(o p j) d -> o p j d", o=HALVES, j=PACK)
 
         acc = {}
 
         def back(o, j, index):
             acc[o, j] = bank(index)
-            cols = slice(j * P, (j + 1) * P)
+            h_codes, h_scales = hq[o, j // 2]
+            cols = slice(j % 2 * P, (j % 2 + 1) * P)
             nc.tensor.matmul_mx(
                 out=acc[o, j][:],
-                lhsT=hq[o][0][:, cols].bitcast(E5M2), lhsT_scale=hq[o][1][:, cols],
+                lhsT=h_codes[:, cols].bitcast(E5M2), lhsT_scale=h_scales[:, cols],
                 rhs=wtq[0][:].bitcast(E4M3), rhs_scale=wtq[1][:],
                 start=True, stop=True,
             )
 
         def empty(o, j, copy, first=0, count=D):
-            copy(
-                out_sb[o][:, j, first : first + count].rearrange("p (c u e) -> p c u e", u=2, e=2),
-                acc[o, j][:].rearrange("p (u c e) -> p c u e", u=2, e=2)[:, first // PACK : (first + count) // PACK],
-            )
+            copy(out_sb[o][:, j, first : first + count], acc[o, j][:, first : first + count])
 
         def store_out(o, j, count):
             nc.sync.dma_start(out_view[o, :, j : j + count, :], out_sb[o][:, j : j + count, :])
 
         o_codes = [keep.tile([P, D], U32, name=f"o_codes{o}", align_bytes=64) for o in range(HALVES)]
         o_scales = keep.tile([P, HALVES, D], U8, name="o_scales", align_bytes=64)
-        o_il = [keep.tile([P, D, PACK], BF16, name=f"o_il{o}", align_bytes=64) for o in range(HALVES)]
+        o_il = {}
 
-        def round_out(o, first, count, copy):
+        def rounded(o, first, count, place=None):
+            name = f"o_il{o}_{first}"
+            o_il[o, first] = keep.tile([P, count, PACK], BF16, name=name, tag=place or name, align_bytes=64)
+
+        def round_out(o, first, skip, count, copy):
             copy(
-                o_il[o][:, first : first + count, :].rearrange("p (c i) j -> p c j i", i=4),
-                out_sb[o][:, :, first : first + count].rearrange("p j (c i) -> p c j i", i=4),
+                o_il[o, first][:, skip : skip + count, :].rearrange("p (c i) j -> p c j i", i=4),
+                out_sb[o][:, :, first + skip : first + skip + count].rearrange("p j (c i) -> p c j i", i=4),
             )
 
-        def quantize_out(o, first, count):
-            quantize((o_codes[o], o_scales[:, o, :]), o_il[o][:, first : first + count, :], E4M3, first, count)
+        def quantize_out(o, first, skip, count):
+            quantize((o_codes[o], o_scales[:, o, :]), o_il[o, first][:, skip : skip + count, :], E4M3, first + skip, count)
 
         def store_codes(o, first=0, count=D):
             nc.sync.dma_start(
@@ -254,90 +276,98 @@ def tile_attend_gnce_pl_x_ts_kernel(tc, xT, wT, y, wt, ts, offs, out_0, out_1, o
 
         gather_w(0)
         gather_w(1)
+        weave_w(0)
         turn_w(0, 6)
         gather_w(2)
         gather_w(3)
-        quantize_w(0, PAIR)
-        quantize_w(PAIR, PAIR)
+        weave_w(1)
+        quantize_w(0, HALF)
         turn_w(1, 3)
         deal_x(0, 0, on_vector)
-        deal_x(0, 1, on_vector)
+        deal_x(0, 1, on_scalar)
+        deal_y(0, 0, on_scalar)
         quantize_x(0, 0)
+        quantize_wt("x_il00")
         quantize_x(0, 1)
+        sigmoids(0, 0, 2, "y_raw00")
         scores(0, 0, (0, 1, 6, 7))
         scores(0, 1, (4, 5))
-        deal_x(1, 0, on_vector)
-        quantize_wt(0, "x_il01")
-        quantize_x(1, 0)
-        deal_y(0, 0, on_vector)
         turn_y(0, 0, 2)
         turn_y(0, 1, 3)
-        deal_x(1, 1, on_vector, "y_raw00")
+        deal_x(1, 0, on_vector)
+        deal_x(1, 1, on_vector)
         deal_y(0, 1, on_scalar)
-        scores(1, 0, (0, 1))
-        subtract(0, 0)
-        quantize_wt(1)
-        subtract(0, 1)
+        quantize_x(1, 0)
+        subtract(0, 0, "x_raw1")
         quantize_x(1, 1)
+        subtract(0, 1)
+        sigmoids(1, 0, 1, "y_raw01")
+        scores(1, 0, (0, 1))
         turn_y(0, 2, 4)
         turn_y(0, 3, 5)
         weigh(0, 0)
         weigh(0, 1)
-        deal_y(1, 0, on_scalar)
-        deal_y(1, 1, on_scalar)
-        scores(1, 1, (0, 1))
-        subtract(0, 2)
         quantize_h(0, 0, 2)
-        back(0, 0, 6)
-        back(0, 1, 7)
-        turn_y(1, 0, 2)
-        turn_y(1, 1, 3)
+        deal_y(1, 0, on_scalar)
+        subtract(0, 2)
         subtract(0, 3)
+        back(0, 0, 4)
+        back(0, 1, 5)
+        results(0, "y_raw10")
         empty(0, 0, on_scalar)
         empty(0, 1, on_scalar)
         store_out(0, 0, 2)
+        deal_y(1, 1, on_scalar)
+        sigmoids(1, 1, 1, "y_raw11")
+        scores(1, 1, (0, 1))
+        turn_y(1, 0, 2)
+        turn_y(1, 1, 3)
         weigh(0, 2)
         weigh(0, 3)
-        turn_y(1, 2, 4)
-        turn_y(1, 3, 5)
-        subtract(1, 0)
         quantize_h(0, 2, 2)
+        subtract(1, 0)
+        subtract(1, 1)
+        turn_y(1, 2, 6)
+        turn_y(1, 3, 7)
         back(0, 2, 0)
         back(0, 3, 1)
         empty(0, 2, on_scalar)
         empty(0, 3, on_scalar)
         store_out(0, 2, 2)
-        subtract(1, 1)
+        rounded(0, 0, PAIR)
+        round_out(0, 0, 0, PAIR, on_scalar)
         weigh(1, 0)
         weigh(1, 1)
-        subtract(1, 2)
         quantize_h(1, 0, 2)
+        subtract(1, 2)
+        subtract(1, 3)
         back(1, 0, 6)
         back(1, 1, 7)
+        results(1)
         empty(1, 0, on_scalar)
         empty(1, 1, on_scalar)
         store_out(1, 0, 2)
-        round_out(0, 0, PAIR, on_scalar)
-        subtract(1, 3)
         weigh(1, 2)
         weigh(1, 3)
         quantize_h(1, 2, 1)
         quantize_h(1, 3, 1)
-        back(1, 2, 0)
-        back(1, 3, 1)
-        round_out(0, PAIR, PAIR, on_vector)
-        quantize_out(0, 0, PAIR)
-        quantize_out(0, PAIR, PAIR)
+        back(1, 2, 2)
+        back(1, 3, 3)
+        rounded(0, PAIR, PAIR, "h_il11")
+        quantize_out(0, 0, 0, PAIR)
+        round_out(0, PAIR, 0, PAIR, on_vector)
         empty(1, 2, on_scalar)
-        store_codes(0)
         store_out(1, 2, 1)
         empty(1, 3, on_vector, 0, PAIR)
+        quantize_out(0, PAIR, 0, PAIR)
+        store_codes(0)
         empty(1, 3, on_vector, PAIR, PAIR)
         store_out(1, 3, 1)
-        round_out(1, 0, 160, on_scalar)
-        round_out(1, 160, 96, on_vector)
-        round_out(1, PAIR, PAIR, on_vector)
-        quantize_out(1, 0, PAIR)
-        quantize_out(1, PAIR, PAIR)
+        rounded(1, 0, D)
+        round_out(1, 0, 0, 160, on_scalar)
+        round_out(1, 0, 160, 96, on_vector)
+        round_out(1, 0, PAIR, PAIR, on_vector)
+        quantize_out(1, 0, 0, PAIR)
+        quantize_out(1, 0, PAIR, PAIR)
         store_codes(1)
         store_scales()

@@ -22,7 +22,6 @@ PACK = 4
 HALF = P * PACK
 HALVES = R // HALF
 PAIR = 2 * P
-W0_FIRST = 1536
 
 
 def tile_attend_gnce_pl_x_ts_kernel(tc, xT, wT, y, wt, ts, offs, out_0, out_1, out_2):
@@ -45,12 +44,14 @@ def tile_attend_gnce_pl_x_ts_kernel(tc, xT, wT, y, wt, ts, offs, out_0, out_1, o
         y_raw = [[keep.tile([P, 2, N], F32, name=f"y_raw{o}{a}", tag=f"y_raw{o}{a}", align_bytes=64) for a in range(2)] for o in range(HALVES)]
 
         ts_row = keep.tile([P, T], F32, name="ts_row")
-        nc.vector.memset(ts_row[:], 0.0)
-        wt_sb = keep.tile([P, HALVES, PACK], F32, name="wt_sb")
-        nc.scalar.dma_start(wt_sb[:], wt[0].rearrange("(o p j) e -> p o (j e)", o=HALVES, j=PACK))
-        nc.sync.dma_start(w_raw[0][:, 0:W0_FIRST], w_view[:, 0, 0:W0_FIRST])
+        nc.vector.memset(ts_row[:, 0 : T // 2], 0.0)
+        nc.gpsimd.memset(ts_row[:, T // 2 : T], 0.0)
+        wt_view = wt[0].rearrange("(o p j) e -> o p (j e)", o=HALVES, j=PACK)
+        wt_sb = [keep.tile([P, PACK], F32, name=f"wt_sb{o}") for o in range(HALVES)]
+        for o in range(HALVES):
+            nc.scalar.dma_start(wt_sb[o][:], wt_view[o])
+        nc.sync.dma_start(w_raw[0][:], w_view[:, 0, :])
         nc.sync.dma_start(ts_row[0:1, :], ts[0:1, :])
-        nc.sync.dma_start(w_raw[0][:, W0_FIRST:T], w_view[:, 0, W0_FIRST:T])
         for t in range(1, PACK):
             nc.sync.dma_start(w_raw[t][:], w_view[:, t, :])
 
@@ -108,7 +109,7 @@ def tile_attend_gnce_pl_x_ts_kernel(tc, xT, wT, y, wt, ts, offs, out_0, out_1, o
         for o in range(HALVES):
             wt_bank = bank(o)
             for j in range(PACK):
-                nc.tensor.transpose(wt_bank[:, j * P : (j + 1) * P], wt_sb[:, o, j : j + 1].to_broadcast([P, P]), ident[:])
+                nc.tensor.transpose(wt_bank[:, j * P : (j + 1) * P], wt_sb[o][:, j : j + 1].to_broadcast([P, P]), ident[:])
             for t in range(PACK):
                 nc.scalar.activation(tw[o][:, t, :], wt_bank[:], ACT.Copy, scale=ts_col[:, t : t + 1])
 

@@ -43,9 +43,8 @@ def tile_attend_gnce_pl_x_ts_kernel(tc, xT, wT, y, wt, ts, offs, out_0, out_1, o
         w_raw = [keep.tile([P, T], F32, name=f"w_raw{t}") for t in range(PACK)]
         y_raw = [[keep.tile([P, 2, N], F32, name=f"y_raw{o}{a}", tag=f"y_raw{o}{a}", align_bytes=64) for a in range(2)] for o in range(HALVES)]
 
-        ts_row = keep.tile([P, T], F32, name="ts_row")
-        nc.vector.memset(ts_row[:, 0 : T // 2], 0.0)
-        nc.gpsimd.memset(ts_row[:, T // 2 : T], 0.0)
+        ts_row = keep.tile([P, T], F32, name="ts_row", tag="ts_row")
+        nc.vector.memset(ts_row[:], 0.0)
         wt_view = wt[0].rearrange("(o p j) e -> o p (j e)", o=HALVES, j=PACK)
         wt_sb = [keep.tile([P, PACK], F32, name=f"wt_sb{o}") for o in range(HALVES)]
         for o in range(HALVES):
@@ -115,8 +114,8 @@ def tile_attend_gnce_pl_x_ts_kernel(tc, xT, wT, y, wt, ts, offs, out_0, out_1, o
 
         w_il = keep.tile([P, N, PACK], BF16, name="w_il", align_bytes=64)
         w_dealt = w_il[:].rearrange("p (r s) t -> p s t r", r=PACK)
-        listed = [keep.tile([P, 2, N], BF16, name=f"listed{u}") for u in range(2)]
-        wt_il = keep.tile([P, D, PACK], BF16, name="wt_il", align_bytes=64)
+        listed = [keep.tile([P, 2, N], BF16, name=f"listed{u}", tag=("ts_row", "listed1")[u]) for u in range(2)]
+        wt_il = keep.tile([P, D, PACK], BF16, name="wt_il", tag="wt_il", align_bytes=64)
         wt_words = wt_il[:].rearrange("s d r -> s (d r)").bitcast(F32).rearrange("s (p t v) -> s p t v", t=PACK, v=2)
         wtq = []
         wq = mx_tiles("wq", N)
@@ -275,6 +274,14 @@ def tile_attend_gnce_pl_x_ts_kernel(tc, xT, wT, y, wt, ts, offs, out_0, out_1, o
 
         on_vector, on_scalar = nc.vector.tensor_copy, nc.scalar.copy
 
+        def warm_up(index):
+            nc.tensor.matmul_mx(
+                out=bank(index)[:],
+                lhsT=wq[0][:, 0:P].bitcast(E4M3), lhsT_scale=wq[1][:, 0:P],
+                rhs=wq[0][:].bitcast(E4M3), rhs_scale=wq[1][:],
+                start=True, stop=True,
+            )
+
         gather_w(0)
         gather_w(1)
         weave_w(0)
@@ -284,49 +291,51 @@ def tile_attend_gnce_pl_x_ts_kernel(tc, xT, wT, y, wt, ts, offs, out_0, out_1, o
         weave_w(1)
         quantize_w(0, HALF)
         turn_w(1, 3)
+        warm_up(4)
+        warm_up(5)
         deal_x(0, 0, on_vector)
         deal_x(0, 1, on_scalar)
         deal_y(0, 0, on_scalar)
         quantize_x(0, 0)
         quantize_wt("x_il00")
         quantize_x(0, 1)
-        sigmoids(0, 0, 2, "y_raw00")
+        sigmoids(0, 0, 1, "y_raw00")
         scores(0, 0, (0, 1, 6, 7))
-        scores(0, 1, (4, 5))
         turn_y(0, 0, 2)
         turn_y(0, 1, 3)
         deal_x(1, 0, on_vector)
-        deal_x(1, 1, on_vector)
-        deal_y(0, 1, on_scalar)
+        deal_x(1, 1, on_scalar)
+        sigmoids(0, 1, 1, "x_raw1")
+        scores(0, 1, (0, 1))
         quantize_x(1, 0)
-        subtract(0, 0, "x_raw1")
-        quantize_x(1, 1)
+        subtract(0, 0, "x_il10")
         subtract(0, 1)
-        sigmoids(1, 0, 1, "y_raw01")
-        scores(1, 0, (0, 1))
         turn_y(0, 2, 4)
         turn_y(0, 3, 5)
+        sigmoids(1, 0, 1, None)
+        scores(1, 0, (6, 7))
         weigh(0, 0)
         weigh(0, 1)
+        quantize_x(1, 1)
         quantize_h(0, 0, 2)
         deal_y(1, 0, on_scalar)
+        sigmoids(1, 1, 1, "y_raw10")
+        scores(1, 1, (0, 1))
+        deal_y(1, 1, on_scalar)
         subtract(0, 2)
         subtract(0, 3)
         back(0, 0, 4)
         back(0, 1, 5)
-        results(0, "y_raw10")
+        results(0, "y_raw11")
         empty(0, 0, on_scalar)
         empty(0, 1, on_scalar)
         store_out(0, 0, 2)
-        deal_y(1, 1, on_scalar)
-        sigmoids(1, 1, 1, "y_raw11")
-        scores(1, 1, (0, 1))
         turn_y(1, 0, 2)
         turn_y(1, 1, 3)
         weigh(0, 2)
         weigh(0, 3)
-        quantize_h(0, 2, 2)
         subtract(1, 0)
+        quantize_h(0, 2, 2)
         subtract(1, 1)
         turn_y(1, 2, 6)
         turn_y(1, 3, 7)
@@ -336,11 +345,11 @@ def tile_attend_gnce_pl_x_ts_kernel(tc, xT, wT, y, wt, ts, offs, out_0, out_1, o
         empty(0, 3, on_scalar)
         store_out(0, 2, 2)
         rounded(0, 0, PAIR)
-        round_out(0, 0, 0, PAIR, on_scalar)
+        round_out(0, 0, 0, P, on_scalar)
         weigh(1, 0)
         weigh(1, 1)
-        quantize_h(1, 0, 2)
         subtract(1, 2)
+        quantize_h(1, 0, 2)
         subtract(1, 3)
         back(1, 0, 6)
         back(1, 1, 7)
@@ -348,6 +357,7 @@ def tile_attend_gnce_pl_x_ts_kernel(tc, xT, wT, y, wt, ts, offs, out_0, out_1, o
         empty(1, 0, on_scalar)
         empty(1, 1, on_scalar)
         store_out(1, 0, 2)
+        round_out(0, 0, P, P, on_scalar)
         weigh(1, 2)
         weigh(1, 3)
         quantize_h(1, 2, 1)
@@ -355,14 +365,14 @@ def tile_attend_gnce_pl_x_ts_kernel(tc, xT, wT, y, wt, ts, offs, out_0, out_1, o
         back(1, 2, 2)
         back(1, 3, 3)
         rounded(0, PAIR, PAIR, "h_il11")
-        quantize_out(0, 0, 0, PAIR)
         round_out(0, PAIR, 0, PAIR, on_vector)
         empty(1, 2, on_scalar)
         store_out(1, 2, 1)
         empty(1, 3, on_vector, 0, PAIR)
         quantize_out(0, PAIR, 0, PAIR)
-        store_codes(0)
         empty(1, 3, on_vector, PAIR, PAIR)
+        quantize_out(0, 0, 0, PAIR)
+        store_codes(0)
         store_out(1, 3, 1)
         rounded(1, 0, D)
         round_out(1, 0, 0, 160, on_scalar)

@@ -34,7 +34,6 @@ def tile_attend_gnce_pl_x_ts_kernel(tc, xT, wT, y, wt, ts, offs, out_0, out_1, o
             return psum.tile([P, HALF], F32, name=f"bank{index}", tag=f"bank{index}")
 
         offsets = keep.tile([P, N // 16], U16, name="offsets")
-        nc.sync.dma_start(offsets[:], offs)
 
         x_view = xT[0].rearrange("(p t) r -> p t r", t=PACK)
         w_view = wT.rearrange("(p t) c -> p t c", t=PACK)
@@ -50,6 +49,7 @@ def tile_attend_gnce_pl_x_ts_kernel(tc, xT, wT, y, wt, ts, offs, out_0, out_1, o
         for o in range(HALVES):
             nc.scalar.dma_start(wt_sb[o][:], wt_view[o])
         nc.sync.dma_start(w_raw[0][:], w_view[:, 0, :])
+        nc.sync.dma_start(offsets[:], offs)
         nc.sync.dma_start(ts_row[0:1, :], ts[0:1, :])
         for t in range(1, PACK):
             nc.sync.dma_start(w_raw[t][:], w_view[:, t, :])
@@ -145,8 +145,11 @@ def tile_attend_gnce_pl_x_ts_kernel(tc, xT, wT, y, wt, ts, offs, out_0, out_1, o
         y_dealt = {}
 
         def deal_y(o, a, copy, place=None):
-            y_dealt[o, a] = keep.tile([P, 2, PACK, P], F32, name=f"y_dealt{o}{a}", tag=place or f"y_dealt{o}{a}", align_bytes=64)
-            copy(y_dealt[o, a][:].rearrange("p j t s -> p j s t"), y_raw[o][a][:].rearrange("p j (s t) -> p j s t", t=PACK))
+            y_dealt[o, a] = keep.tile([P, PACK, PAIR], F32, name=f"y_dealt{o}{a}", tag=place or f"y_dealt{o}{a}", align_bytes=64)
+            copy(
+                y_dealt[o, a][:].rearrange("p t (c i) -> p c t i", i=2),
+                y_raw[o][a][:].rearrange("p j (c i t) -> p (j c) t i", i=2, t=PACK),
+            )
 
         y_turned = {}
 
@@ -154,7 +157,7 @@ def tile_attend_gnce_pl_x_ts_kernel(tc, xT, wT, y, wt, ts, offs, out_0, out_1, o
             yt = y_turned[o, j] = bank(index)
             a, jj = divmod(j, 2)
             for t in range(PACK):
-                rows = y_dealt[o, a][:, jj, t, :] if (o, a) in y_dealt else y_raw[o][a][:, jj, t:N:PACK]
+                rows = y_dealt[o, a][:, t, jj * P : (jj + 1) * P] if (o, a) in y_dealt else y_raw[o][a][:, jj, t:N:PACK]
                 nc.tensor.transpose(yt[:, t * P : (t + 1) * P], rows, ident[:])
 
         sigs = {}
@@ -202,9 +205,9 @@ def tile_attend_gnce_pl_x_ts_kernel(tc, xT, wT, y, wt, ts, offs, out_0, out_1, o
                 h_il[o, a] = keep.tile([P, PAIR, PACK], BF16, name=f"h_il{o}{a}", tag=place or f"h_il{o}{a}", align_bytes=64)
             cols = slice(jj * P, (jj + count) * P)
             nc.vector.tensor_tensor(
-                h_il[o, a][:, cols, :].rearrange("p (c i) t -> p c t i", i=4),
-                diff[o, a][:, :, cols].rearrange("p t (c i) -> p c t i", i=4),
-                tw[o][:, :, j * P : (j + count) * P].rearrange("p t (c i) -> p c t i", i=4),
+                h_il[o, a][:, cols, :].rearrange("p (c i) t -> p c t i", i=2),
+                diff[o, a][:, :, cols].rearrange("p t (c i) -> p c t i", i=2),
+                tw[o][:, :, j * P : (j + count) * P].rearrange("p t (c i) -> p c t i", i=2),
                 ALU.mult,
             )
 
@@ -252,8 +255,8 @@ def tile_attend_gnce_pl_x_ts_kernel(tc, xT, wT, y, wt, ts, offs, out_0, out_1, o
 
         def round_out(o, first, skip, count, copy):
             copy(
-                o_il[o, first][:, skip : skip + count, :].rearrange("p (c i) j -> p c j i", i=4),
-                out_sb[o][:, :, first + skip : first + skip + count].rearrange("p j (c i) -> p c j i", i=4),
+                o_il[o, first][:, skip : skip + count, :].rearrange("p (c i) j -> p c j i", i=2),
+                out_sb[o][:, :, first + skip : first + skip + count].rearrange("p j (c i) -> p c j i", i=2),
             )
 
         def quantize_out(o, first, skip, count):

@@ -322,30 +322,31 @@ def tile_attend_gnce_pl_x_ts_kernel(tc, xT, wT, y, wt, ts, offs, out_0, out_1, o
         quantize_x(1, 1)
         quantize_h(0, 0, 2)
         deal_y(1, 0, on_scalar)
-        sigmoids(1, 1, 1, "y_raw10")
-        scores(1, 1, (0, 1))
         deal_y(1, 1, on_scalar)
+        sigmoids(1, 1, 1, "y_raw11")
+        scores(1, 1, (0, 1, 6, 7))
         subtract(0, 2)
         subtract(0, 3)
-        back(0, 0, 4)
-        back(0, 1, 5)
-        results(0, "y_raw11")
+        turn_y(1, 0, 2)
+        turn_y(1, 1, 3)
+        turn_y(1, 2, 4)
+        turn_y(1, 3, 5)
+        back(0, 0, 0)
+        back(0, 1, 1)
+        results(0)
         empty(0, 0, on_scalar)
         empty(0, 1, on_scalar)
         store_out(0, 0, 2)
-        turn_y(1, 0, 2)
-        turn_y(1, 1, 3)
         weigh(0, 2)
         weigh(0, 3)
         subtract(1, 0)
         quantize_h(0, 2, 2)
         subtract(1, 1)
-        turn_y(1, 2, 6)
-        turn_y(1, 3, 7)
-        back(0, 2, 0)
-        back(0, 3, 1)
+        back(0, 2, 6)
+        back(0, 3, 7)
         empty(0, 2, on_scalar)
-        empty(0, 3, on_scalar)
+        empty(0, 3, on_scalar, 0, PAIR)
+        empty(0, 3, on_scalar, PAIR, PAIR)
         store_out(0, 2, 2)
         rounded(0, 0, PAIR)
         round_out(0, 0, 0, P, on_scalar)
@@ -354,8 +355,8 @@ def tile_attend_gnce_pl_x_ts_kernel(tc, xT, wT, y, wt, ts, offs, out_0, out_1, o
         subtract(1, 2)
         quantize_h(1, 0, 2)
         subtract(1, 3)
-        back(1, 0, 6)
-        back(1, 1, 7)
+        back(1, 0, 4)
+        back(1, 1, 5)
         results(1)
         empty(1, 0, on_scalar)
         empty(1, 1, on_scalar)

@@ -277,14 +277,6 @@ def tile_attend_gnce_pl_x_ts_kernel(tc, xT, wT, y, wt, ts, offs, out_0, out_1, o
 
         on_vector, on_scalar = nc.vector.tensor_copy, nc.scalar.copy
 
-        def warm_up(index):
-            nc.tensor.matmul_mx(
-                out=bank(index)[:],
-                lhsT=wq[0][:, 0:P].bitcast(E4M3), lhsT_scale=wq[1][:, 0:P],
-                rhs=wq[0][:].bitcast(E4M3), rhs_scale=wq[1][:],
-                start=True, stop=True,
-            )
-
         gather_w(0)
         gather_w(1)
         weave_w(0)
@@ -294,8 +286,6 @@ def tile_attend_gnce_pl_x_ts_kernel(tc, xT, wT, y, wt, ts, offs, out_0, out_1, o
         weave_w(1)
         quantize_w(0, HALF)
         turn_w(1, 3)
-        warm_up(4)
-        warm_up(5)
         deal_x(0, 0, on_vector)
         deal_x(0, 1, on_scalar)
         deal_y(0, 0, on_scalar)
@@ -348,7 +338,7 @@ def tile_attend_gnce_pl_x_ts_kernel(tc, xT, wT, y, wt, ts, offs, out_0, out_1, o
         empty(0, 3, on_scalar, 0, PAIR)
         empty(0, 3, on_scalar, PAIR, PAIR)
         store_out(0, 2, 2)
-        rounded(0, 0, PAIR)
+        rounded(0, 0, P)
         round_out(0, 0, 0, P, on_scalar)
         weigh(1, 0)
         weigh(1, 1)
@@ -361,27 +351,28 @@ def tile_attend_gnce_pl_x_ts_kernel(tc, xT, wT, y, wt, ts, offs, out_0, out_1, o
         empty(1, 0, on_scalar)
         empty(1, 1, on_scalar)
         store_out(1, 0, 2)
-        round_out(0, 0, P, P, on_scalar)
         weigh(1, 2)
         weigh(1, 3)
         quantize_h(1, 2, 1)
         quantize_h(1, 3, 1)
         back(1, 2, 2)
         back(1, 3, 3)
-        rounded(0, PAIR, PAIR, "h_il11")
-        round_out(0, PAIR, 0, PAIR, on_vector)
+        rounded(0, P, 3 * P, "h_il11")
+        round_out(0, P, 0, PAIR, on_vector)
+        round_out(0, P, PAIR, P, on_vector)
+        quantize_out(0, 0, 0, P)
+        quantize_out(0, P, 0, PAIR)
+        quantize_out(0, P, PAIR, P)
         empty(1, 2, on_scalar)
         store_out(1, 2, 1)
-        empty(1, 3, on_vector, 0, PAIR)
-        quantize_out(0, PAIR, 0, PAIR)
-        empty(1, 3, on_vector, PAIR, PAIR)
-        quantize_out(0, 0, 0, PAIR)
         store_codes(0)
+        empty(1, 3, on_scalar, 0, PAIR)
+        empty(1, 3, on_scalar, PAIR, PAIR)
         store_out(1, 3, 1)
         rounded(1, 0, D)
-        round_out(1, 0, 0, 160, on_scalar)
-        round_out(1, 0, 160, 96, on_vector)
-        round_out(1, 0, PAIR, PAIR, on_vector)
+        round_out(1, 0, 0, PAIR, on_vector)
+        round_out(1, 0, PAIR, P, on_scalar)
+        round_out(1, 0, 3 * P, P, on_vector)
         quantize_out(1, 0, 0, PAIR)
         quantize_out(1, 0, PAIR, PAIR)
         store_codes(1)

@@ -23,6 +23,8 @@ HALF = P * PACK
 HALVES = R // HALF
 PAIR = 2 * P
 
+VECTOR_GATHERS = 320
+
 
 def tile_attend_gnce_pl_x_ts_kernel(tc, xT, wT, y, wt, ts, offs, out_0, out_1, out_2):
     nc = tc.nc
@@ -96,6 +98,12 @@ def tile_attend_gnce_pl_x_ts_kernel(tc, xT, wT, y, wt, ts, offs, out_0, out_1, o
             xq[o, a] = mx_tiles(f"xq{o}{a}", PAIR)
             quantize(xq[o, a], x_il[o, a][:], E4M3, 0, PAIR)
 
+        wt_banks = [bank(o) for o in range(HALVES)]
+        for o in range(HALVES):
+            for j in range(PACK):
+                nc.tensor.transpose(wt_banks[o][:, j * P : (j + 1) * P], wt_sb[o][:, j : j + 1].to_broadcast([P, P]), ident[:])
+        wt_spread = keep.tile([P, HALF], F32, name="wt_spread")
+        nc.scalar.copy(wt_spread[:], wt_banks[1][:])
         ts_listed = keep.tile([P, N], F32, name="ts_listed")
         nc.vector.tensor_copy(ts_listed[:], ts_row[:].indirect(offsets[:]))
         ts_bank = bank(2)
@@ -105,12 +113,10 @@ def tile_attend_gnce_pl_x_ts_kernel(tc, xT, wT, y, wt, ts, offs, out_0, out_1, o
         nc.scalar.copy(ts_col[:], ts_bank[:, 0:HALF:P])
 
         tw = [keep.tile([P, PACK, HALF], F32, name=f"tw{o}") for o in range(HALVES)]
-        for o in range(HALVES):
-            wt_bank = bank(o)
-            for j in range(PACK):
-                nc.tensor.transpose(wt_bank[:, j * P : (j + 1) * P], wt_sb[o][:, j : j + 1].to_broadcast([P, P]), ident[:])
-            for t in range(PACK):
-                nc.scalar.activation(tw[o][:, t, :], wt_bank[:], ACT.Copy, scale=ts_col[:, t : t + 1])
+        for t in range(PACK):
+            nc.scalar.activation(tw[0][:, t, :], wt_banks[0][:], ACT.Copy, scale=ts_col[:, t : t + 1])
+        for t in range(PACK):
+            nc.gpsimd.tensor_scalar(tw[1][:, t, :], wt_spread[:], ts_col[:, t : t + 1], 0.0, ALU.mult, ALU.add)
 
         w_il = keep.tile([P, N, PACK], BF16, name="w_il", align_bytes=64)
         w_dealt = w_il[:].rearrange("p (r s) t -> p s t r", r=PACK)
@@ -123,8 +129,14 @@ def tile_attend_gnce_pl_x_ts_kernel(tc, xT, wT, y, wt, ts, offs, out_0, out_1, o
         def gather_w(t):
             nc.vector.tensor_copy(listed[t // 2][:, t % 2, :], w_raw[t][:].indirect(offsets[:]))
 
-        def weave_w(u):
-            nc.vector.tensor_copy(w_dealt[:, :, 2 * u : 2 * u + 2, :], listed[u][:].rearrange("p t (s r) -> p s t r", r=PACK))
+        def gather_w_shared(t):
+            cut = VECTOR_GATHERS // 16
+            nc.vector.tensor_copy(listed[t // 2][:, t % 2, :VECTOR_GATHERS], w_raw[t][:].indirect(offsets[:, :cut]))
+            nc.scalar.activation(listed[t // 2][:, t % 2, VECTOR_GATHERS:], w_raw[t][:].indirect(offsets[:, cut:]), ACT.Copy)
+
+        def weave_w(u, first=0, count=PACK):
+            planes = slice(first, first + count)
+            nc.vector.tensor_copy(w_dealt[:, :, 2 * u : 2 * u + 2, planes], listed[u][:].rearrange("p t (s r) -> p s t r", r=PACK)[:, :, :, planes])
 
         def turn_w(u, index):
             turned = bank(index)
@@ -282,9 +294,11 @@ def tile_attend_gnce_pl_x_ts_kernel(tc, xT, wT, y, wt, ts, offs, out_0, out_1, o
         weave_w(0)
         turn_w(0, 6)
         gather_w(2)
-        gather_w(3)
-        weave_w(1)
-        quantize_w(0, HALF)
+        gather_w_shared(3)
+        weave_w(1, 0, 2)
+        weave_w(1, 2, 2)
+        quantize_w(0, PAIR)
+        quantize_w(PAIR, PAIR)
         turn_w(1, 3)
         deal_x(0, 0, on_vector)
         deal_x(0, 1, on_scalar)

@@ -23,14 +23,35 @@ HALF = P * PACK
 HALVES = R // HALF
 PAIR = 2 * P
 
-VECTOR_GATHERS = 320
+KIB = 1024
+PLACES = {
+    "wt_il1": "x_raw0",
+    "x_il10": 6 * KIB,
+    "xq00_codes": 3 * KIB // 2,
+    "y_dealt_single3": 0 * KIB,
+    "x_il11": 2 * KIB,
+    "sig01": "x_raw1",
+    "y_dealt11": "xq10_codes",
+    "sig11": "y_raw11",
+    "y_dealt10": "xq01_codes",
+    "x_il00": 5 * KIB,
+    "wtq_codes": 4 * KIB,
+}
 
 
 def tile_attend_gnce_pl_x_ts_kernel(tc, xT, wT, y, wt, ts, offs, out_0, out_1, out_2):
     nc = tc.nc
     with ExitStack() as ctx:
         keep = ctx.enter_context(tc.tile_pool(name="keep", bufs=1))
+        shared = ctx.enter_context(tc.tile_pool(name="shared", bufs=1))
         psum = ctx.enter_context(tc.psum_pool(name="psum", bufs=1))
+
+        def tile(name, shape, dtype, place=None):
+            if place is None:
+                place = PLACES.get(name, name)
+            if isinstance(place, int):
+                return shared.tile([P] + shape, dtype, name=name, align_bytes=64, offset=place)
+            return keep.tile([P] + shape, dtype, name=name, tag=place, align_bytes=64)
 
         def bank(index):
             return psum.tile([P, HALF], F32, name=f"bank{index}", tag=f"bank{index}")
@@ -40,9 +61,9 @@ def tile_attend_gnce_pl_x_ts_kernel(tc, xT, wT, y, wt, ts, offs, out_0, out_1, o
         x_view = xT[0].rearrange("(p t) r -> p t r", t=PACK)
         w_view = wT.rearrange("(p t) c -> p t c", t=PACK)
         y_view = y[0].rearrange("(o p j) i -> o p j i", o=HALVES, j=PACK)
-        x_raw = [keep.tile([P, PACK, HALF], F32, name=f"x_raw{o}", tag=f"x_raw{o}", align_bytes=64) for o in range(HALVES)]
+        x_raw = [tile(f"x_raw{o}", [PACK, HALF], F32) for o in range(HALVES)]
         w_raw = [keep.tile([P, T], F32, name=f"w_raw{t}") for t in range(PACK)]
-        y_raw = [[keep.tile([P, 2, N], F32, name=f"y_raw{o}{a}", tag=f"y_raw{o}{a}", align_bytes=64) for a in range(2)] for o in range(HALVES)]
+        y_raw = {(o, a): tile(f"y_raw{o}{a}", [2, N], F32) for o in range(HALVES) for a in range(2) if o}
 
         ts_row = keep.tile([P, T], F32, name="ts_row", tag="ts_row")
         nc.vector.memset(ts_row[:], 0.0)
@@ -60,12 +81,19 @@ def tile_attend_gnce_pl_x_ts_kernel(tc, xT, wT, y, wt, ts, offs, out_0, out_1, o
             nc.sync.dma_start(x_raw[o][:], x_view[:, :, o * HALF : (o + 1) * HALF])
 
         def load_y(o, a):
-            nc.sync.dma_start(y_raw[o][a][:], y_view[o, :, 2 * a : 2 * a + 2, :])
+            nc.sync.dma_start(y_raw[o, a][:], y_view[o, :, 2 * a : 2 * a + 2, :])
+
+        y_single = [tile(f"y_single{j}", [N], F32) for j in range(PACK)]
+
+        def load_y_tile(j):
+            nc.sync.dma_start(y_single[j][:], y_view[0, :, j, :])
 
         load_x(0)
-        load_y(0, 0)
+        load_y_tile(0)
         load_x(1)
-        load_y(0, 1)
+        load_y_tile(1)
+        load_y_tile(2)
+        load_y_tile(3)
         load_y(1, 0)
         load_y(1, 1)
 
@@ -75,7 +103,7 @@ def tile_attend_gnce_pl_x_ts_kernel(tc, xT, wT, y, wt, ts, offs, out_0, out_1, o
         nc.scalar.activation(warm[:], ident[:, 0:1], ACT.Sigmoid)
 
         def mx_tiles(name, width, place=None):
-            codes = keep.tile([P, width], U32, name=name + "_codes", tag=place or name + "_codes", align_bytes=64)
+            codes = tile(name + "_codes", [width], U32, place)
             scales = keep.tile([P, width], U8, name=name + "_scales", align_bytes=64)
             return codes, scales
 
@@ -88,14 +116,14 @@ def tile_attend_gnce_pl_x_ts_kernel(tc, xT, wT, y, wt, ts, offs, out_0, out_1, o
         xq = {}
 
         def deal_x(o, a, copy, place=None):
-            x_il[o, a] = keep.tile([P, PAIR, PACK], BF16, name=f"x_il{o}{a}", tag=place or f"x_il{o}{a}", align_bytes=64)
+            x_il[o, a] = tile(f"x_il{o}{a}", [PAIR, PACK], BF16, place)
             copy(
                 x_il[o, a][:].rearrange("p (j s) t -> p s t j", j=2),
                 x_raw[o][:].rearrange("p t (s j) -> p s t j", j=PACK)[:, :, :, 2 * a : 2 * a + 2],
             )
 
-        def quantize_x(o, a):
-            xq[o, a] = mx_tiles(f"xq{o}{a}", PAIR)
+        def quantize_x(o, a, place=None):
+            xq[o, a] = mx_tiles(f"xq{o}{a}", PAIR, place)
             quantize(xq[o, a], x_il[o, a][:], E4M3, 0, PAIR)
 
         wt_banks = [bank(o) for o in range(HALVES)]
@@ -121,22 +149,21 @@ def tile_attend_gnce_pl_x_ts_kernel(tc, xT, wT, y, wt, ts, offs, out_0, out_1, o
         w_il = keep.tile([P, N, PACK], BF16, name="w_il", align_bytes=64)
         w_dealt = w_il[:].rearrange("p (r s) t -> p s t r", r=PACK)
         listed = [keep.tile([P, 2, N], BF16, name=f"listed{u}", tag=("ts_row", "listed1")[u]) for u in range(2)]
-        wt_il = keep.tile([P, D, PACK], BF16, name="wt_il", tag="wt_il", align_bytes=64)
-        wt_words = wt_il[:].rearrange("s d r -> s (d r)").bitcast(F32).rearrange("s (p t v) -> s p t v", t=PACK, v=2)
-        wtq = []
+        wt_il = {}
+        wtq = mx_tiles("wtq", D)
         wq = mx_tiles("wq", N)
 
         def gather_w(t):
             nc.vector.tensor_copy(listed[t // 2][:, t % 2, :], w_raw[t][:].indirect(offsets[:]))
 
-        def gather_w_shared(t):
-            cut = VECTOR_GATHERS // 16
-            nc.vector.tensor_copy(listed[t // 2][:, t % 2, :VECTOR_GATHERS], w_raw[t][:].indirect(offsets[:, :cut]))
-            nc.scalar.activation(listed[t // 2][:, t % 2, VECTOR_GATHERS:], w_raw[t][:].indirect(offsets[:, cut:]), ACT.Copy)
+        def weave_w(u):
+            nc.vector.tensor_copy(w_dealt[:, :, 2 * u : 2 * u + 2, :], listed[u][:].rearrange("p t (s r) -> p s t r", r=PACK))
 
-        def weave_w(u, first=0, count=PACK):
-            planes = slice(first, first + count)
-            nc.vector.tensor_copy(w_dealt[:, :, 2 * u : 2 * u + 2, planes], listed[u][:].rearrange("p t (s r) -> p s t r", r=PACK)[:, :, :, planes])
+        def gather_woven(t):
+            nc.vector.tensor_copy(w_dealt[:, :, t, :], w_raw[t][:].indirect(offsets[:]))
+
+        def unweave_w(t):
+            nc.scalar.copy(listed[t // 2][:, t % 2, :].rearrange("p (s r) -> p s r", r=PACK), w_dealt[:, :, t, :])
 
         def turn_w(u, index):
             turned = bank(index)
@@ -145,22 +172,34 @@ def tile_attend_gnce_pl_x_ts_kernel(tc, xT, wT, y, wt, ts, offs, out_0, out_1, o
                 for v in range(2):
                     col = (2 * tt + v) * P
                     nc.tensor.transpose(turned[:, col : col + P], words[:, v : N // 2 : 2], ident[:])
-            nc.scalar.copy(wt_words[:, :, 2 * u : 2 * u + 2, :], turned[:].rearrange("s (t v p) -> s p t v", t=2, v=2))
+            wt_il[u] = tile(f"wt_il{u}", [PAIR, PACK], BF16)
+            nc.scalar.copy(
+                wt_il[u][:].rearrange("s d r -> s (d r)").bitcast(F32).rearrange("s (p t v) -> s p t v", t=2, v=2),
+                turned[:].rearrange("s (t v p) -> s p t v", t=2, v=2),
+            )
 
         def quantize_w(first, count):
             quantize(wq, w_il[:, first : first + count, :], E4M3, first, count)
 
-        def quantize_wt(place=None):
-            wtq.extend(mx_tiles("wtq", D, place))
-            quantize(wtq, wt_il[:], E4M3, 0, D)
+        def quantize_wt(u):
+            quantize(wtq, wt_il[u][:], E4M3, u * PAIR, PAIR)
 
         y_dealt = {}
 
         def deal_y(o, a, copy, place=None):
-            y_dealt[o, a] = keep.tile([P, PACK, PAIR], F32, name=f"y_dealt{o}{a}", tag=place or f"y_dealt{o}{a}", align_bytes=64)
+            y_dealt[o, a] = tile(f"y_dealt{o}{a}", [PACK, PAIR], F32, place)
             copy(
                 y_dealt[o, a][:].rearrange("p t (c i) -> p c t i", i=2),
-                y_raw[o][a][:].rearrange("p j (c i t) -> p (j c) t i", i=2, t=PACK),
+                y_raw[o, a][:].rearrange("p j (c i t) -> p (j c) t i", i=2, t=PACK),
+            )
+
+        y_dealt_single = {}
+
+        def deal_y_tile(j, copy):
+            y_dealt_single[j] = tile(f"y_dealt_single{j}", [PACK, P], F32)
+            copy(
+                y_dealt_single[j][:].rearrange("p t (c i) -> p c t i", i=2),
+                y_single[j][:].rearrange("p (c i t) -> p c t i", i=2, t=PACK),
             )
 
         y_turned = {}
@@ -169,16 +208,21 @@ def tile_attend_gnce_pl_x_ts_kernel(tc, xT, wT, y, wt, ts, offs, out_0, out_1, o
             yt = y_turned[o, j] = bank(index)
             a, jj = divmod(j, 2)
             for t in range(PACK):
-                rows = y_dealt[o, a][:, t, jj * P : (jj + 1) * P] if (o, a) in y_dealt else y_raw[o][a][:, jj, t:N:PACK]
+                if o:
+                    rows = y_dealt[o, a][:, t, jj * P : (jj + 1) * P]
+                elif j in y_dealt_single:
+                    rows = y_dealt_single[j][:, t, :]
+                else:
+                    rows = y_single[j][:, t:N:PACK]
                 nc.tensor.transpose(yt[:, t * P : (t + 1) * P], rows, ident[:])
 
         sigs = {}
 
         def sigmoids(o, first, count, place):
             name = f"sig{o}{first}"
-            tile = keep.tile([P, count, PACK, PAIR], F32, name=name, tag=place or name, align_bytes=64)
+            made = tile(name, [count, PACK, PAIR], F32, place)
             for a in range(count):
-                sigs[o, first + a] = tile[:, a]
+                sigs[o, first + a] = made[:, a]
 
         def scores(o, a, banks):
             sig = sigs[o, a]
@@ -203,7 +247,7 @@ def tile_attend_gnce_pl_x_ts_kernel(tc, xT, wT, y, wt, ts, offs, out_0, out_1, o
         def subtract(o, j, place=None):
             a, jj = divmod(j, 2)
             if (o, a) not in diff:
-                diff[o, a] = keep.tile([P, PACK, PAIR], F32, name=f"diff{o}{a}", tag=place or f"diff{o}{a}", align_bytes=64)
+                diff[o, a] = tile(f"diff{o}{a}", [PACK, PAIR], F32, place)
             cols = slice(jj * P, (jj + 1) * P)
             nc.vector.tensor_tensor(
                 diff[o, a][:, :, cols], sigs[o, a][:, :, cols], y_turned[o, j][:].rearrange("p (t c) -> p t c", t=PACK), ALU.subtract
@@ -214,7 +258,7 @@ def tile_attend_gnce_pl_x_ts_kernel(tc, xT, wT, y, wt, ts, offs, out_0, out_1, o
         def weigh(o, j, count=1, place=None):
             a, jj = divmod(j, 2)
             if (o, a) not in h_il:
-                h_il[o, a] = keep.tile([P, PAIR, PACK], BF16, name=f"h_il{o}{a}", tag=place or f"h_il{o}{a}", align_bytes=64)
+                h_il[o, a] = tile(f"h_il{o}{a}", [PAIR, PACK], BF16, place)
             cols = slice(jj * P, (jj + count) * P)
             nc.vector.tensor_tensor(
                 h_il[o, a][:, cols, :].rearrange("p (c i) t -> p c t i", i=2),
@@ -234,7 +278,7 @@ def tile_attend_gnce_pl_x_ts_kernel(tc, xT, wT, y, wt, ts, offs, out_0, out_1, o
         out_sb = {}
 
         def results(o, place=None):
-            out_sb[o] = keep.tile([P, PACK, D], F32, name=f"out_sb{o}", tag=place or f"out_sb{o}", align_bytes=64)
+            out_sb[o] = tile(f"out_sb{o}", [PACK, D], F32, place)
 
         out_view = out_0[0].rearrange("(o p j) d -> o p j d", o=HALVES, j=PACK)
 
@@ -252,7 +296,11 @@ def tile_attend_gnce_pl_x_ts_kernel(tc, xT, wT, y, wt, ts, offs, out_0, out_1, o
             )
 
         def empty(o, j, copy, first=0, count=D):
-            copy(out_sb[o][:, j, first : first + count], acc[o, j][:, first : first + count])
+            features = slice(first // PACK, (first + count) // PACK)
+            copy(
+                out_sb[o][:, j, :].rearrange("s (p u t) -> s p u t", u=2, t=2)[:, features],
+                acc[o, j][:].rearrange("s (u p t) -> s p u t", u=2, t=2)[:, features],
+            )
 
         def store_out(o, j, count):
             nc.sync.dma_start(out_view[o, :, j : j + count, :], out_sb[o][:, j : j + count, :])
@@ -263,7 +311,7 @@ def tile_attend_gnce_pl_x_ts_kernel(tc, xT, wT, y, wt, ts, offs, out_0, out_1, o
 
         def rounded(o, first, count, place=None):
             name = f"o_il{o}_{first}"
-            o_il[o, first] = keep.tile([P, count, PACK], BF16, name=name, tag=place or name, align_bytes=64)
+            o_il[o, first] = tile(name, [count, PACK], BF16, place)
 
         def round_out(o, first, skip, count, copy):
             copy(
@@ -293,43 +341,44 @@ def tile_attend_gnce_pl_x_ts_kernel(tc, xT, wT, y, wt, ts, offs, out_0, out_1, o
         gather_w(1)
         weave_w(0)
         turn_w(0, 6)
-        gather_w(2)
-        gather_w_shared(3)
-        weave_w(1, 0, 2)
-        weave_w(1, 2, 2)
-        quantize_w(0, PAIR)
-        quantize_w(PAIR, PAIR)
-        turn_w(1, 3)
+        gather_woven(2)
+        unweave_w(2)
+        gather_woven(3)
+        quantize_w(0, HALF)
+        unweave_w(3)
         deal_x(0, 0, on_vector)
         deal_x(0, 1, on_scalar)
-        deal_y(0, 0, on_scalar)
+        deal_y_tile(0, on_scalar)
+        turn_w(1, 3)
         quantize_x(0, 0)
-        quantize_wt("x_il00")
         quantize_x(0, 1)
-        sigmoids(0, 0, 1, "y_raw00")
+        quantize_wt(0)
+        quantize_wt(1)
+        sigmoids(0, 0, 1, None)
         scores(0, 0, (0, 1, 6, 7))
         turn_y(0, 0, 2)
         turn_y(0, 1, 3)
         deal_x(1, 0, on_vector)
         deal_x(1, 1, on_scalar)
-        sigmoids(0, 1, 1, "x_raw1")
-        scores(0, 1, (0, 1))
+        sigmoids(0, 1, 1, None)
+        scores(0, 1, (6, 7))
+        deal_y_tile(3, on_scalar)
+        subtract(0, 0)
         quantize_x(1, 0)
-        subtract(0, 0, "x_il10")
+        weigh(0, 0)
         subtract(0, 1)
         turn_y(0, 2, 4)
         turn_y(0, 3, 5)
+        deal_y(1, 0, on_scalar)
         sigmoids(1, 0, 1, None)
         scores(1, 0, (6, 7))
-        weigh(0, 0)
-        weigh(0, 1)
         quantize_x(1, 1)
-        quantize_h(0, 0, 2)
-        deal_y(1, 0, on_scalar)
+        weigh(0, 1)
         deal_y(1, 1, on_scalar)
-        sigmoids(1, 1, 1, "y_raw11")
+        sigmoids(1, 1, 1, None)
         scores(1, 1, (0, 1, 6, 7))
         subtract(0, 2)
+        quantize_h(0, 0, 2)
         subtract(0, 3)
         turn_y(1, 0, 2)
         turn_y(1, 1, 3)

@@ -23,6 +23,8 @@ HALF = P * PACK
 HALVES = R // HALF
 PAIR = 2 * P
 
+VECTOR_GATHERS = 320
+SCALAR_TABLES = 3
 KIB = 1024
 PLACES = {
     "wt_il1": "x_raw0",
@@ -30,9 +32,7 @@ PLACES = {
     "xq00_codes": 3 * KIB // 2,
     "y_dealt_single3": 0 * KIB,
     "x_il11": 2 * KIB,
-    "sig01": "x_raw1",
     "y_dealt11": "xq10_codes",
-    "sig11": "y_raw11",
     "y_dealt10": "xq01_codes",
     "x_il00": 5 * KIB,
     "wtq_codes": 4 * KIB,
@@ -104,7 +104,7 @@ def tile_attend_gnce_pl_x_ts_kernel(tc, xT, wT, y, wt, ts, offs, out_0, out_1, o
 
         def mx_tiles(name, width, place=None):
             codes = tile(name + "_codes", [width], U32, place)
-            scales = keep.tile([P, width], U8, name=name + "_scales", align_bytes=64)
+            scales = tile(name + "_scales", [width], U8)
             return codes, scales
 
         def quantize(planes, src, fmt, first, count):
@@ -115,11 +115,13 @@ def tile_attend_gnce_pl_x_ts_kernel(tc, xT, wT, y, wt, ts, offs, out_0, out_1, o
         x_il = {}
         xq = {}
 
-        def deal_x(o, a, copy, place=None):
-            x_il[o, a] = tile(f"x_il{o}{a}", [PAIR, PACK], BF16, place)
+        def deal_x(o, a, copy, first=0, count=P):
+            if (o, a) not in x_il:
+                x_il[o, a] = tile(f"x_il{o}{a}", [PAIR, PACK], BF16)
+            rows = slice(first, first + count)
             copy(
-                x_il[o, a][:].rearrange("p (j s) t -> p s t j", j=2),
-                x_raw[o][:].rearrange("p t (s j) -> p s t j", j=PACK)[:, :, :, 2 * a : 2 * a + 2],
+                x_il[o, a][:].rearrange("p (j s) t -> p s t j", j=2)[:, rows],
+                x_raw[o][:].rearrange("p t (s j) -> p s t j", j=PACK)[:, rows, :, 2 * a : 2 * a + 2],
             )
 
         def quantize_x(o, a, place=None):
@@ -130,42 +132,46 @@ def tile_attend_gnce_pl_x_ts_kernel(tc, xT, wT, y, wt, ts, offs, out_0, out_1, o
         for o in range(HALVES):
             for j in range(PACK):
                 nc.tensor.transpose(wt_banks[o][:, j * P : (j + 1) * P], wt_sb[o][:, j : j + 1].to_broadcast([P, P]), ident[:])
-        wt_spread = keep.tile([P, HALF], F32, name="wt_spread")
-        nc.scalar.copy(wt_spread[:], wt_banks[1][:])
+        wt_spread = [keep.tile([P, HALF], F32, name=f"wt_spread{o}") for o in range(HALVES)]
+        for o in range(HALVES):
+            nc.scalar.copy(wt_spread[o][:], wt_banks[o][:])
         ts_listed = keep.tile([P, N], F32, name="ts_listed")
         nc.vector.tensor_copy(ts_listed[:], ts_row[:].indirect(offsets[:]))
-        ts_bank = bank(2)
-        for t in range(PACK):
-            nc.tensor.transpose(ts_bank[:, t * P : (t + 1) * P], ts_listed[:, t:N:PACK], ident[:])
         ts_col = keep.tile([P, PACK], F32, name="ts_col")
-        nc.scalar.copy(ts_col[:], ts_bank[:, 0:HALF:P])
+        for t in range(PACK):
+            ts_bank = bank(2 + t)
+            nc.tensor.transpose(ts_bank[:, :P], ts_listed[:, t:N:PACK], ident[:])
+            nc.scalar.copy(ts_col[:, t : t + 1], ts_bank[:, 0:1])
 
         tw = [keep.tile([P, PACK, HALF], F32, name=f"tw{o}") for o in range(HALVES)]
         for t in range(PACK):
-            nc.scalar.activation(tw[0][:, t, :], wt_banks[0][:], ACT.Copy, scale=ts_col[:, t : t + 1])
-        for t in range(PACK):
-            nc.gpsimd.tensor_scalar(tw[1][:, t, :], wt_spread[:], ts_col[:, t : t + 1], 0.0, ALU.mult, ALU.add)
+            for o in range(HALVES):
+                if o == 0 and t < SCALAR_TABLES:
+                    nc.scalar.activation(tw[o][:, t, :], wt_banks[o][:], ACT.Copy, scale=ts_col[:, t : t + 1])
+                else:
+                    nc.gpsimd.tensor_scalar(tw[o][:, t, :], wt_spread[o][:], ts_col[:, t : t + 1], 0.0, ALU.mult, ALU.add)
 
         w_il = keep.tile([P, N, PACK], BF16, name="w_il", align_bytes=64)
         w_dealt = w_il[:].rearrange("p (r s) t -> p s t r", r=PACK)
-        listed = [keep.tile([P, 2, N], BF16, name=f"listed{u}", tag=("ts_row", "listed1")[u]) for u in range(2)]
+        listed_row = keep.tile([P, PACK * N], BF16, name="listed_row", tag="ts_row")
+        listed = [listed_row[:, 2 * u * N : 2 * (u + 1) * N].rearrange("p (t c) -> p t c", t=2) for u in range(2)]
         wt_il = {}
-        wtq = mx_tiles("wtq", D)
+        wtq = []
         wq = mx_tiles("wq", N)
 
         def gather_w(t):
             nc.vector.tensor_copy(listed[t // 2][:, t % 2, :], w_raw[t][:].indirect(offsets[:]))
 
-        def weave_w(u):
-            nc.vector.tensor_copy(w_dealt[:, :, 2 * u : 2 * u + 2, :], listed[u][:].rearrange("p t (s r) -> p s t r", r=PACK))
+        def gather_w_shared(t):
+            cut = VECTOR_GATHERS // 16
+            nc.vector.tensor_copy(listed[t // 2][:, t % 2, :VECTOR_GATHERS], w_raw[t][:].indirect(offsets[:, :cut]))
+            nc.scalar.activation(listed[t // 2][:, t % 2, VECTOR_GATHERS:], w_raw[t][:].indirect(offsets[:, cut:]), ACT.Copy)
 
-        def gather_woven(t):
-            nc.vector.tensor_copy(w_dealt[:, :, t, :], w_raw[t][:].indirect(offsets[:]))
+        def weave_w(copy, first, count):
+            tiles = slice(first, first + count)
+            copy(w_dealt[:, :, :, tiles], listed_row[:].rearrange("p (t s r) -> p s t r", t=PACK, r=PACK)[:, :, :, tiles])
 
-        def unweave_w(t):
-            nc.scalar.copy(listed[t // 2][:, t % 2, :].rearrange("p (s r) -> p s r", r=PACK), w_dealt[:, :, t, :])
-
-        def turn_w(u, index):
+        def turn_w(u, index, copy):
             turned = bank(index)
             for tt in range(2):
                 words = listed[u][:, tt, :].bitcast(F32)
@@ -173,7 +179,7 @@ def tile_attend_gnce_pl_x_ts_kernel(tc, xT, wT, y, wt, ts, offs, out_0, out_1, o
                     col = (2 * tt + v) * P
                     nc.tensor.transpose(turned[:, col : col + P], words[:, v : N // 2 : 2], ident[:])
             wt_il[u] = tile(f"wt_il{u}", [PAIR, PACK], BF16)
-            nc.scalar.copy(
+            copy(
                 wt_il[u][:].rearrange("s d r -> s (d r)").bitcast(F32).rearrange("s (p t v) -> s p t v", t=2, v=2),
                 turned[:].rearrange("s (t v p) -> s p t v", t=2, v=2),
             )
@@ -182,6 +188,8 @@ def tile_attend_gnce_pl_x_ts_kernel(tc, xT, wT, y, wt, ts, offs, out_0, out_1, o
             quantize(wq, w_il[:, first : first + count, :], E4M3, first, count)
 
         def quantize_wt(u):
+            if not wtq:
+                wtq.extend(mx_tiles("wtq", D))
             quantize(wtq, wt_il[u][:], E4M3, u * PAIR, PAIR)
 
         y_dealt = {}
@@ -339,17 +347,18 @@ def tile_attend_gnce_pl_x_ts_kernel(tc, xT, wT, y, wt, ts, offs, out_0, out_1, o
 
         gather_w(0)
         gather_w(1)
-        weave_w(0)
-        turn_w(0, 6)
-        gather_woven(2)
-        unweave_w(2)
-        gather_woven(3)
-        quantize_w(0, HALF)
-        unweave_w(3)
+        turn_w(0, 6, on_vector)
+        gather_w(2)
+        gather_w_shared(3)
+        weave_w(on_vector, 0, 2)
+        weave_w(on_vector, 2, 1)
+        weave_w(on_scalar, 3, 1)
+        quantize_w(0, PAIR)
         deal_x(0, 0, on_vector)
+        quantize_w(PAIR, PAIR)
         deal_x(0, 1, on_scalar)
         deal_y_tile(0, on_scalar)
-        turn_w(1, 3)
+        turn_w(1, 3, on_scalar)
         quantize_x(0, 0)
         quantize_x(0, 1)
         quantize_wt(0)
@@ -359,7 +368,8 @@ def tile_attend_gnce_pl_x_ts_kernel(tc, xT, wT, y, wt, ts, offs, out_0, out_1, o
         turn_y(0, 0, 2)
         turn_y(0, 1, 3)
         deal_x(1, 0, on_vector)
-        deal_x(1, 1, on_scalar)
+        deal_x(1, 1, on_vector, 0, P // 2)
+        deal_x(1, 1, on_scalar, P // 2, P // 2)
         sigmoids(0, 1, 1, None)
         scores(0, 1, (6, 7))
         deal_y_tile(3, on_scalar)
@@ -388,8 +398,9 @@ def tile_attend_gnce_pl_x_ts_kernel(tc, xT, wT, y, wt, ts, offs, out_0, out_1, o
         back(0, 1, 1)
         results(0)
         empty(0, 0, on_scalar)
+        store_out(0, 0, 1)
         empty(0, 1, on_scalar)
-        store_out(0, 0, 2)
+        store_out(0, 1, 1)
         weigh(0, 2)
         weigh(0, 3)
         subtract(1, 0)
@@ -398,9 +409,10 @@ def tile_attend_gnce_pl_x_ts_kernel(tc, xT, wT, y, wt, ts, offs, out_0, out_1, o
         back(0, 2, 6)
         back(0, 3, 7)
         empty(0, 2, on_scalar)
+        store_out(0, 2, 1)
         empty(0, 3, on_scalar, 0, PAIR)
         empty(0, 3, on_scalar, PAIR, PAIR)
-        store_out(0, 2, 2)
+        store_out(0, 3, 1)
         rounded(0, 0, P)
         round_out(0, 0, 0, P, on_scalar)
         weigh(1, 0)
@@ -412,8 +424,9 @@ def tile_attend_gnce_pl_x_ts_kernel(tc, xT, wT, y, wt, ts, offs, out_0, out_1, o
         back(1, 1, 5)
         results(1)
         empty(1, 0, on_scalar)
+        store_out(1, 0, 1)
         empty(1, 1, on_scalar)
-        store_out(1, 0, 2)
+        store_out(1, 1, 1)
         weigh(1, 2)
         weigh(1, 3)
         quantize_h(1, 2, 1)
@@ -437,6 +450,7 @@ def tile_attend_gnce_pl_x_ts_kernel(tc, xT, wT, y, wt, ts, offs, out_0, out_1, o
         round_out(1, 0, PAIR, P, on_scalar)
         round_out(1, 0, 3 * P, P, on_vector)
         quantize_out(1, 0, 0, PAIR)
+        store_codes(1, 0, PAIR)
         quantize_out(1, 0, PAIR, PAIR)
-        store_codes(1)
+        store_codes(1, PAIR, PAIR)
         store_scales()

from contextlib import ExitStack

import concourse.mybir as mybir
from concourse.masks import make_identity

N, T, D, R = 512, 2048, 512, 1024
FLOPS = 2 * 2 * R * N * D

F32 = mybir.dt.float32
BF16 = mybir.dt.bfloat16
U32 = mybir.dt.uint32
I32 = mybir.dt.int32
U16 = mybir.dt.uint16
U8 = mybir.dt.uint8
E4M3 = mybir.dt.float8_e4m3fn_x4
E5M2 = mybir.dt.float8_e5m2_x4
ACT = mybir.ActivationFunctionType
ALU = mybir.AluOpType

P = 128
PACK = 4
HALF = P * PACK
HALVES = R // HALF
PAIR = 2 * P

VECTOR_GATHERS = 320
SCALAR_TABLES = 3
KIB = 1024
PLACES = {
    "wt_il1": "x_raw0",
    "x_il10": 6 * KIB,
    "xq00_codes": 3 * KIB // 2,
    "y_dealt_single3": 0 * KIB,
    "x_il11": 2 * KIB,
    "y_dealt11": "xq10_codes",
    "y_dealt10": "xq01_codes",
    "x_il00": 5 * KIB,
    "wtq_codes": 4 * KIB,
}


def tile_attend_gnce_pl_x_ts_kernel(tc, xT, wT, y, wt, ts, offs, out_0, out_1, out_2):
    nc = tc.nc
    with ExitStack() as ctx:
        keep = ctx.enter_context(tc.tile_pool(name="keep", bufs=1))
        shared = ctx.enter_context(tc.tile_pool(name="shared", bufs=1))
        psum = ctx.enter_context(tc.psum_pool(name="psum", bufs=1))

        def tile(name, shape, dtype, place=None):
            if place is None:
                place = PLACES.get(name, name)
            if isinstance(place, int):
                return shared.tile([P] + shape, dtype, name=name, align_bytes=64, offset=place)
            return keep.tile([P] + shape, dtype, name=name, tag=place, align_bytes=64)

        def bank(index):
            return psum.tile([P, HALF], F32, name=f"bank{index}", tag=f"bank{index}")

        offsets = keep.tile([P, N // 16], U16, name="offsets")

        x_view = xT[0].rearrange("(p t) r -> p t r", t=PACK)
        w_view = wT.rearrange("(p t) c -> p t c", t=PACK)
        y_view = y[0].rearrange("(o p j) i -> o p j i", o=HALVES, j=PACK)
        x_raw = [tile(f"x_raw{o}", [PACK, HALF], F32) for o in range(HALVES)]
        w_raw = [keep.tile([P, T], F32, name=f"w_raw{t}") for t in range(PACK)]
        y_raw = {(o, a): tile(f"y_raw{o}{a}", [2, N], F32) for o in range(HALVES) for a in range(2) if o}

        ts_row = keep.tile([P, T], F32, name="ts_row", tag="ts_row")
        nc.vector.memset(ts_row[:], 0.0)
        wt_view = wt[0].rearrange("(o p j) e -> o p (j e)", o=HALVES, j=PACK)
        wt_sb = [keep.tile([P, PACK], F32, name=f"wt_sb{o}") for o in range(HALVES)]
        for o in range(HALVES):
            nc.scalar.dma_start(wt_sb[o][:], wt_view[o])
        nc.sync.dma_start(w_raw[0][:], w_view[:, 0, :])
        nc.sync.dma_start(offsets[:], offs)
        nc.sync.dma_start(ts_row[0:1, :], ts[0:1, :])
        for t in range(1, PACK):
            nc.sync.dma_start(w_raw[t][:], w_view[:, t, :])

        def load_x(o):
            nc.sync.dma_start(x_raw[o][:], x_view[:, :, o * HALF : (o + 1) * HALF])

        def load_y(o, a):
            nc.sync.dma_start(y_raw[o, a][:], y_view[o, :, 2 * a : 2 * a + 2, :])

        y_single = [tile(f"y_single{j}", [N], F32) for j in range(PACK)]

        def load_y_tile(j):
            nc.sync.dma_start(y_single[j][:], y_view[0, :, j, :])

        load_x(0)
        load_y_tile(0)
        load_x(1)
        load_y_tile(1)
        load_y_tile(2)
        load_y_tile(3)
        load_y(1, 0)
        load_y(1, 1)

        ident = keep.tile([P, P], F32, name="ident")
        make_identity(nc, ident[:])
        warm = keep.tile([P, 1], F32, name="warm")
        nc.scalar.activation(warm[:], ident[:, 0:1], ACT.Sigmoid)

        def mx_tiles(name, width, place=None):
            codes = tile(name + "_codes", [width], U32, place)
            scales = tile(name + "_scales", [width], U8)
            return codes, scales

        def quantize(planes, src, fmt, first, count):
            codes, scales = planes
            cols = slice(first, first + count)
            nc.vector.quantize_mx(out=codes[:, cols].bitcast(fmt), scales=scales[:, cols], in_=src.rearrange("p c t -> p (c t)"))

        x_il = {}
        xq = {}

        def deal_x(o, a, copy, first=0, count=P):
            if (o, a) not in x_il:
                x_il[o, a] = tile(f"x_il{o}{a}", [PAIR, PACK], BF16)
            rows = slice(first, first + count)
            copy(
                x_il[o, a][:].rearrange("p (j s) t -> p s t j", j=2)[:, rows],
                x_raw[o][:].rearrange("p t (s j) -> p s t j", j=PACK)[:, rows, :, 2 * a : 2 * a + 2],
            )

        def quantize_x(o, a, place=None):
            xq[o, a] = mx_tiles(f"xq{o}{a}", PAIR, place)
            quantize(xq[o, a], x_il[o, a][:], E4M3, 0, PAIR)

        wt_banks = [bank(o) for o in range(HALVES)]
        for o in range(HALVES):
            for j in range(PACK):
                nc.tensor.transpose(wt_banks[o][:, j * P : (j + 1) * P], wt_sb[o][:, j : j + 1].to_broadcast([P, P]), ident[:])
        wt_spread = [keep.tile([P, HALF], F32, name=f"wt_spread{o}") for o in range(HALVES)]
        for o in range(HALVES):
            nc.scalar.copy(wt_spread[o][:], wt_banks[o][:])
        ts_listed = keep.tile([P, N], F32, name="ts_listed")
        nc.vector.tensor_copy(ts_listed[:], ts_row[:].indirect(offsets[:]))
        ts_col = keep.tile([P, PACK], F32, name="ts_col")
        for t in range(PACK):
            ts_bank = bank(2 + t)
            nc.tensor.transpose(ts_bank[:, :P], ts_listed[:, t:N:PACK], ident[:])
            nc.scalar.copy(ts_col[:, t : t + 1], ts_bank[:, 0:1])

        tw = [keep.tile([P, PACK, HALF], F32, name=f"tw{o}") for o in range(HALVES)]
        for t in range(PACK):
            for o in range(HALVES):
                if o == 0 and t < SCALAR_TABLES:
                    nc.scalar.activation(tw[o][:, t, :], wt_banks[o][:], ACT.Copy, scale=ts_col[:, t : t + 1])
                else:
                    nc.gpsimd.tensor_scalar(tw[o][:, t, :], wt_spread[o][:], ts_col[:, t : t + 1], 0.0, ALU.mult, ALU.add)

        w_il = keep.tile([P, N, PACK], BF16, name="w_il", align_bytes=64)
        w_dealt = w_il[:].rearrange("p (r s) t -> p s t r", r=PACK)
        listed_row = keep.tile([P, PACK * N], BF16, name="listed_row", tag="ts_row")
        listed = [listed_row[:, 2 * u * N : 2 * (u + 1) * N].rearrange("p (t c) -> p t c", t=2) for u in range(2)]
        wt_il = {}
        wtq = []
        wq = mx_tiles("wq", N)

        def gather_w(t):
            nc.vector.tensor_copy(listed[t // 2][:, t % 2, :], w_raw[t][:].indirect(offsets[:]))

        def gather_w_shared(t):
            cut = VECTOR_GATHERS // 16
            nc.vector.tensor_copy(listed[t // 2][:, t % 2, :VECTOR_GATHERS], w_raw[t][:].indirect(offsets[:, :cut]))
            nc.scalar.activation(listed[t // 2][:, t % 2, VECTOR_GATHERS:], w_raw[t][:].indirect(offsets[:, cut:]), ACT.Copy)

        def weave_w(copy, first, count):
            tiles = slice(first, first + count)
            copy(w_dealt[:, :, :, tiles], listed_row[:].rearrange("p (t s r) -> p s t r", t=PACK, r=PACK)[:, :, :, tiles])

        def turn_w(u, index, copy):
            turned = bank(index)
            for tt in range(2):
                words = listed[u][:, tt, :].bitcast(F32)
                for v in range(2):
                    col = (2 * tt + v) * P
                    nc.tensor.transpose(turned[:, col : col + P], words[:, v : N // 2 : 2], ident[:])
            wt_il[u] = tile(f"wt_il{u}", [PAIR, PACK], BF16)
            copy(
                wt_il[u][:].rearrange("s d r -> s (d r)").bitcast(F32).rearrange("s (p t v) -> s p t v", t=2, v=2),
                turned[:].rearrange("s (t v p) -> s p t v", t=2, v=2),
            )

        def quantize_w(first, count):
            quantize(wq, w_il[:, first : first + count, :], E4M3, first, count)

        def quantize_wt(u):
            if not wtq:
                wtq.extend(mx_tiles("wtq", D))
            quantize(wtq, wt_il[u][:], E4M3, u * PAIR, PAIR)

        y_dealt = {}

        def deal_y(o, a, copy, place=None):
            y_dealt[o, a] = tile(f"y_dealt{o}{a}", [PACK, PAIR], F32, place)
            copy(
                y_dealt[o, a][:].rearrange("p t (c i) -> p c t i", i=2),
                y_raw[o, a][:].rearrange("p j (c i t) -> p (j c) t i", i=2, t=PACK),
            )

        y_dealt_single = {}

        def deal_y_tile(j, copy):
            y_dealt_single[j] = tile(f"y_dealt_single{j}", [PACK, P], F32)
            copy(
                y_dealt_single[j][:].rearrange("p t (c i) -> p c t i", i=2),
                y_single[j][:].rearrange("p (c i t) -> p c t i", i=2, t=PACK),
            )

        y_turned = {}

        def turn_y(o, j, index):
            yt = y_turned[o, j] = bank(index)
            a, jj = divmod(j, 2)
            for t in range(PACK):
                if o:
                    rows = y_dealt[o, a][:, t, jj * P : (jj + 1) * P]
                elif j in y_dealt_single:
                    rows = y_dealt_single[j][:, t, :]
                else:
                    rows = y_single[j][:, t:N:PACK]
                nc.tensor.transpose(yt[:, t * P : (t + 1) * P], rows, ident[:])

        sigs = {}

        def sigmoids(o, first, count, place):
            name = f"sig{o}{first}"
            made = tile(name, [count, PACK, PAIR], F32, place)
            for a in range(count):
                sigs[o, first + a] = made[:, a]

        def scores(o, a, banks):
            sig = sigs[o, a]
            x_codes, x_scales = xq[o, a]
            share = PACK // len(banks)
            for b, index in enumerate(banks):
                sc = bank(index)
                for tt in range(share):
                    slots = slice((share * b + tt) * P, (share * b + tt + 1) * P)
                    nc.tensor.matmul_mx(
                        out=sc[:, tt * PAIR : (tt + 1) * PAIR],
                        lhsT=wq[0][:, slots].bitcast(E4M3), lhsT_scale=wq[1][:, slots],
                        rhs=x_codes[:].bitcast(E4M3), rhs_scale=x_scales[:],
                        start=True, stop=True,
                    )
                for tt in range(share):
                    t = share * b + tt
                    nc.scalar.activation(sig[:, t, :], sc[:, tt * PAIR : (tt + 1) * PAIR], ACT.Sigmoid, scale=ts_col[:, t : t + 1])

        diff = {}

        def subtract(o, j, place=None):
            a, jj = divmod(j, 2)
            if (o, a) not in diff:
                diff[o, a] = tile(f"diff{o}{a}", [PACK, PAIR], F32, place)
            cols = slice(jj * P, (jj + 1) * P)
            nc.vector.tensor_tensor(
                diff[o, a][:, :, cols], sigs[o, a][:, :, cols], y_turned[o, j][:].rearrange("p (t c) -> p t c", t=PACK), ALU.subtract
            )

        h_il = {}

        def weigh(o, j, count=1, place=None):
            a, jj = divmod(j, 2)
            if (o, a) not in h_il:
                h_il[o, a] = tile(f"h_il{o}{a}", [PAIR, PACK], BF16, place)
            cols = slice(jj * P, (jj + count) * P)
            nc.vector.tensor_tensor(
                h_il[o, a][:, cols, :].rearrange("p (c i) t -> p c t i", i=2),
                diff[o, a][:, :, cols].rearrange("p t (c i) -> p c t i", i=2),
                tw[o][:, :, j * P : (j + count) * P].rearrange("p t (c i) -> p c t i", i=2),
                ALU.mult,
            )

        hq = {}

        def quantize_h(o, j, count, place=None):
            a, jj = divmod(j, 2)
            if (o, a) not in hq:
                hq[o, a] = mx_tiles(f"hq{o}{a}", PAIR, place)
            quantize(hq[o, a], h_il[o, a][:, jj * P : (jj + count) * P, :], E5M2, jj * P, count * P)

        out_sb = {}

        def results(o, place=None):
            out_sb[o] = tile(f"out_sb{o}", [PACK, D], F32, place)

        out_view = out_0[0].rearrange("(o p j) d -> o p j d", o=HALVES, j=PACK)

        acc = {}

        def back(o, j, index):
            acc[o, j] = bank(index)
            h_codes, h_scales = hq[o, j // 2]
            cols = slice(j % 2 * P, (j % 2 + 1) * P)
            nc.tensor.matmul_mx(
                out=acc[o, j][:],
                lhsT=h_codes[:, cols].bitcast(E5M2), lhsT_scale=h_scales[:, cols],
                rhs=wtq[0][:].bitcast(E4M3), rhs_scale=wtq[1][:],
                start=True, stop=True,
            )

        def empty(o, j, copy, first=0, count=D):
            features = slice(first // PACK, (first + count) // PACK)
            copy(
                out_sb[o][:, j, :].rearrange("s (p u t) -> s p u t", u=2, t=2)[:, features],
                acc[o, j][:].rearrange("s (u p t) -> s p u t", u=2, t=2)[:, features],
            )

        def store_out(o, j, count):
            nc.sync.dma_start(out_view[o, :, j : j + count, :], out_sb[o][:, j : j + count, :])

        o_codes = [keep.tile([P, D], U32, name=f"o_codes{o}", align_bytes=64) for o in range(HALVES)]
        o_scales = keep.tile([P, HALVES, D], U8, name="o_scales", align_bytes=64)
        o_il = {}

        def rounded(o, first, count, place=None):
            name = f"o_il{o}_{first}"
            o_il[o, first] = tile(name, [count, PACK], BF16, place)

        def round_out(o, first, skip, count, copy):
            copy(
                o_il[o, first][:, skip : skip + count, :].rearrange("p (c i) j -> p c j i", i=2),
                out_sb[o][:, :, first + skip : first + skip + count].rearrange("p j (c i) -> p c j i", i=2),
            )

        def quantize_out(o, first, skip, count):
            quantize((o_codes[o], o_scales[:, o, :]), o_il[o, first][:, skip : skip + count, :], E4M3, first + skip, count)

        def store_codes(o, first=0, count=D):
            nc.sync.dma_start(
                out_1[o].rearrange("p d l -> p (d l)").bitcast(I32)[:, first : first + count], o_codes[o][:, first : first + count].bitcast(I32)
            )

        def store_scales():
            for q in range(4):
                queue = nc.scalar if q % 2 else nc.sync
                queue.dma_start(
                    out_2[:, 4 * q : 4 * q + 4, :].rearrange("o f d -> f o d").bitcast(I32),
                    o_scales[32 * q : 32 * q + 4, :, :].bitcast(I32),
                )

        on_vector, on_scalar = nc.vector.tensor_copy, nc.scalar.copy

        gather_w(0)
        gather_w(1)
        turn_w(0, 6, on_vector)
        gather_w(2)
        gather_w_shared(3)
        weave_w(on_vector, 0, 2)
        weave_w(on_vector, 2, 1)
        weave_w(on_scalar, 3, 1)
        quantize_w(0, PAIR)
        deal_x(0, 0, on_vector)
        quantize_w(PAIR, PAIR)
        deal_x(0, 1, on_scalar)
        deal_y_tile(0, on_scalar)
        turn_w(1, 3, on_scalar)
        quantize_x(0, 0)
        quantize_x(0, 1)
        quantize_wt(0)
        quantize_wt(1)
        sigmoids(0, 0, 1, None)
        scores(0, 0, (0, 1, 6, 7))
        turn_y(0, 0, 2)
        turn_y(0, 1, 3)
        deal_x(1, 0, on_vector)
        deal_x(1, 1, on_vector, 0, P // 2)
        deal_x(1, 1, on_scalar, P // 2, P // 2)
        sigmoids(0, 1, 1, None)
        scores(0, 1, (6, 7))
        deal_y_tile(3, on_scalar)
        subtract(0, 0)
        quantize_x(1, 0)
        weigh(0, 0)
        subtract(0, 1)
        turn_y(0, 2, 4)
        turn_y(0, 3, 5)
        deal_y(1, 0, on_scalar)
        sigmoids(1, 0, 1, None)
        scores(1, 0, (6, 7))
        quantize_x(1, 1)
        weigh(0, 1)
        deal_y(1, 1, on_scalar)
        sigmoids(1, 1, 1, None)
        scores(1, 1, (0, 1, 6, 7))
        subtract(0, 2)
        quantize_h(0, 0, 2)
        subtract(0, 3)
        turn_y(1, 0, 2)
        turn_y(1, 1, 3)
        turn_y(1, 2, 4)
        turn_y(1, 3, 5)
        back(0, 0, 0)
        back(0, 1, 1)
        results(0)
        empty(0, 0, on_scalar)
        store_out(0, 0, 1)
        empty(0, 1, on_scalar)
        store_out(0, 1, 1)
        weigh(0, 2)
        weigh(0, 3)
        subtract(1, 0)
        quantize_h(0, 2, 2)
        subtract(1, 1)
        back(0, 2, 6)
        back(0, 3, 7)
        empty(0, 2, on_scalar)
        store_out(0, 2, 1)
        empty(0, 3, on_scalar, 0, PAIR)
        empty(0, 3, on_scalar, PAIR, PAIR)
        store_out(0, 3, 1)
        rounded(0, 0, P)
        round_out(0, 0, 0, P, on_scalar)
        weigh(1, 0)
        weigh(1, 1)
        subtract(1, 2)
        quantize_h(1, 0, 2)
        subtract(1, 3)
        back(1, 0, 4)
        back(1, 1, 5)
        results(1)
        empty(1, 0, on_scalar)
        store_out(1, 0, 1)
        empty(1, 1, on_scalar)
        store_out(1, 1, 1)
        weigh(1, 2)
        weigh(1, 3)
        quantize_h(1, 2, 1)
        quantize_h(1, 3, 1)
        back(1, 2, 2)
        back(1, 3, 3)
        rounded(0, P, 3 * P, "h_il11")
        round_out(0, P, 0, PAIR, on_vector)
        round_out(0, P, PAIR, P, on_vector)
        quantize_out(0, 0, 0, P)
        quantize_out(0, P, 0, PAIR)
        quantize_out(0, P, PAIR, P)
        empty(1, 2, on_scalar)
        store_out(1, 2, 1)
        store_codes(0)
        empty(1, 3, on_scalar, 0, PAIR)
        empty(1, 3, on_scalar, PAIR, PAIR)
        store_out(1, 3, 1)
        rounded(1, 0, D)
        round_out(1, 0, 0, PAIR, on_vector)
        round_out(1, 0, PAIR, P, on_scalar)
        round_out(1, 0, 3 * P, P, on_vector)
        quantize_out(1, 0, 0, PAIR)
        store_codes(1, 0, PAIR)
        quantize_out(1, 0, PAIR, PAIR)
        store_codes(1, PAIR, PAIR)
        store_scales()
